import numpy as np, ml_dtypes
CORES = [6,15,38,47]
N = 4
BF = ml_dtypes.bfloat16
V, L, M, S, RO, E = 4096, 256, 16, 5, 3, 10
def pack(X, w, Q, T):
    return {"ent": np.ascontiguousarray(np.transpose(X, (0, 1, 3, 2)).reshape(N, 128, V)).astype(np.float32).astype(BF), "hw": np.reshape(w, (N, 128, 1)).astype(np.int32),
            "mix": np.reshape(Q, (N, 128, 16)).astype(np.float32).astype(BF), "goal": np.reshape(T, (N, 128, 1)).astype(np.int32)}
def genes(rng, p):
    return np.where(rng.random((N, 8, V, 16)) < p, rng.integers(1, 256, (N, 8, V, 16)), 0)
def aims(rng, Q):
    return np.matmul(rng.integers(1, 256, (N, 8, 1, 16)), Q)[:, :, 0]
def parts(rng):
    share = rng.choice(np.array([0.2, 0.3, 0.4, 0.55]), (N, 8, 1, 1))
    X = genes(rng, share * (0.5 + rng.random((N, 8, V, 1)))); w = rng.integers(1, 256, (N, 8, 16)); Q = rng.integers(-8, 9, (N, 8, 16, 16))
    return X, w, Q, aims(rng, Q)
def spot(x, w):
    u = np.matmul(x, w) & 4095
    return V // 2 + (((u * u >> 5) + 37 * u) & (V // 2 - 1))
def setup_inputs(rng):
    return pack(*parts(rng))
def setup_inputs_ends(rng):
    share = rng.choice(np.array([0.1, 0.2, 0.4, 0.7]), (N, 8, 1, 1)); share[:, 5] = 0.08; share[:, 6:] = 0.6
    X = 255 * (rng.random((N, 8, V, 16)) < share * (0.5 + rng.random((N, 8, V, 1)))).astype(np.int64)
    w = np.where(rng.random((N, 8, 16)) < 0.5, 1, 255)
    for g in (3, 6): w[:, g] = 255
    for g in (1, 7): w[:, g, :2] = 1; w[:, g, 2] = 255
    Q = 16 * rng.integers(0, 2, (N, 8, 16, 16)) - 8; Q[:, 5:] = 8
    T = 65280 * rng.integers(0, 2, (N, 8, 16)) - 32640; T[:, 5] = -32640
    T[1::2, 7] = -32640; T[0::2, 7] = 32640; T[1::2, 6] = 32640; T[0::2, 6] = -32640
    X[:, :, V - 1] = 255; X[:, :, V - 2] = 0
    for t in range(RO):
        for i in (0, 3, L - 1):
            for g in (1, 7): X[:, g, L * t + i] = 0; X[:, g, L * t + i, :3] = 255
            X[:, 6, L * t + i] = 255
        for i in (2, L - 2): X[:, 7, L * t + i] = 255; X[:, 6, L * t + i] = 0
    return pack(X, w, Q, T)
def setup_inputs_spread(rng):
    p = 1.3 * np.sqrt(rng.random((N, 8, V, 1))) * rng.random((N, 8, 1, 16))
    X = np.where(rng.random((N, 8, V, 16)) < p, np.minimum(np.exp2(8 * rng.random((N, 8, V, 16))).astype(np.int64), 255), 0)
    w = np.minimum(np.exp2(8 * rng.random((N, 8, 16))).astype(np.int64), 255)
    Q = rng.integers(-8, 9, (N, 8, 16, 16)) * (rng.random((N, 8, 16, 16)) < 0.2 + rng.random((N, 8, 16, 1)))
    T = np.clip(((2 * rng.random((N, 8, 16)) - 1) * np.exp2(10 + 5 * rng.random((N, 8, 16)))).astype(np.int64), -32640, 32640)
    return pack(X, w, Q, T)
def setup_inputs_corners(rng):
    X, w, Q, T = parts(rng); H = V // 2; full = rng.integers(1, 256, (N, 8, V, 16)); one = np.arange(16)[None, :] == rng.integers(0, 16, (H, 1))
    for r in range(N):
        for g in range(8):
            k = (g + r) % 8
            if k == 0: X[r, g] = full[r, g]
            if k == 1: X[r, g] = np.where(rng.random((V, 16)) < 0.02, full[r, g], 0)
            if k == 2: w[r, g] = 1
            if k == 3: w[r, g] = 255
            if k == 4: X[r, g, :H] = full[r, g, :H]; X[r, g, H:] = 0
            if k == 5: X[r, g, :H] = np.where(one, full[r, g, :H], 0); X[r, g, H:] = full[r, g, H:]
            if k == 6: Q[r, g] = 0; T[r, g] = 0
            if k == 7: X[r, g, :H, :8] = full[r, g, :H, :8]; X[r, g, :H, 8:] = 0; X[r, g, H:, :8] = 0; X[r, g, H:, 8:] = full[r, g, H:, 8:]
    return pack(X, w, Q, T)
def setup_inputs_alike(rng):
    X, w, Q, T = parts(rng); n = rng.choice(np.array([4, 12, 40]), (N, 8, 1)); n[:, 0] = 4; n[:, 1] = 40
    pick = (n * rng.random((N, 8, V))).astype(np.int64)
    return pack(np.take_along_axis(X[:, :, :40], np.minimum(pick, n - 1)[..., None], 2), w, Q, T)
def setup_inputs_close(rng):
    X, w, Q, T = parts(rng); H = V // 2; K = RO * L
    F = int(rng.integers(0, N)); Z = (F + 1) % N
    X[F] = rng.integers(1, 256, (8, V, 16))
    sub = np.zeros((16384, 16), np.int64); sub[:, 0] = 255; sub[:, 1:15] = 255 * ((np.arange(16384)[:, None] >> np.arange(14)[None, :]) & 1)
    for r in range(N):
        for g in range(8):
            s = int(rng.choice(np.array([-1, 1])))
            if g in (0, 7):
                Q[r, g, 0] = 0; Q[r, g, 0, 0] = -s; Q[r, g, 1:5] = -8 * s; Q[r, g, 5:] = s * rng.integers(0, 3, (11, 16)); T[r, g] = 32640 * s
            elif g in (1, 2):
                Q[r, g] = 8 * s; Q[r, g, 0, 1:] = 0; T[r, g] = 32640 * s; T[r, g, 0] = -32640 * s
            elif g == 3:
                z = rng.choice(np.array([-1, 1]), 16); Q[r, g] = 8 * z; T[r, g] = -32640 * z
            else:
                Q[r, g] = 8; T[r, g] = 32640
            if r == F: continue
            if g == 3:
                X[r, g, :K] = 255; X[r, g, :K, :15] -= rng.integers(0, 2, (K, 15))
                X[r, g, H:] = 254; X[r, g, H:, :15] -= rng.integers(0, 2, (H, 15))
                continue
            c = sub[15::16] if g in (0, 7) else sub
            X[r, g, H:] = 255; X[r, g, H:, 0] = 254 if g in (0, 7) else rng.integers(240 if g < 3 else 192, 255, H)
            if r == Z and g in (4, 5, 6):
                c = np.array(c); c[:, 0] = 254; X[r, g, H:, 0] = 255
            b = spot(c, w[r, g]); o = rng.permutation(np.unique(b, return_index=True)[1])
            e = np.concatenate([o, rng.choice(o[1:], L)])[:L]
            if g in (0, 7): e[0] = np.argmax(b)
            if g == 4: e[:] = e[0]
            if g == 6: e[L - 1] = e[0]
            X[r, g, :K] = c[rng.choice(o, K)]; X[r, g, :L] = c[e]
    return pack(X, w, Q, T)
def check_inputs(d):
    bad = []
    for k, lo, hi in (("ent", 0, 255), ("hw", 1, 255), ("mix", -8, 8), ("goal", -32640, 32640)):
        v = np.asarray(d[k]).astype(np.float64)
        if not np.all((v >= lo) & (v <= hi)): bad.append("range of " + k)
        elif np.any(v != np.floor(v)): bad.append("whole numbers of " + k)
    return bad
def reference(ent, hw, mix, goal):
    X = np.ascontiguousarray(np.transpose(np.asarray(ent).astype(np.float32).reshape(N, 8, 16, V), (0, 1, 3, 2)))
    w = hw.astype(np.float32).reshape(N, 8, 16, 1); Q = mix.astype(np.float32).reshape(N, 8, 16, 16); T = goal.astype(np.float32).reshape(N, 8, 1, 16)
    gr = np.arange(8)[:, None]; m = np.tile(np.arange(M), L); low = np.tri(L, L, -1, dtype=bool)
    def hash12(s, z): return np.matmul(z, w[s])[..., 0].astype(np.int64) & 4095
    def misfit(s, z): return np.add.reduce(np.abs(np.matmul(z, Q[s]) - T[s]), axis=-1)
    for t in range(RO):
        new = np.array(X)
        for r in range(N):
            q = (r + 1 + t % (N - 1)) % N
            A = X[r, :, L * t:L * t + L]; u = hash12(r, A)
            b = V // 2 + (((u * u >> 5) + 37 * u) & (V // 2 - 1)); B = X[r][gr, b]; AB = np.where(A == 0, B, A)
            first = np.logical_not(np.any((b[:, :, None] == b[:, None, :]) & low, axis=2))
            A2 = np.repeat(A, M, axis=1); B2 = np.repeat(B, M, axis=1); AB2 = np.repeat(AB, M, axis=1); c = np.zeros_like(A2)
            for d in range(S):
                v = hash12(q, np.where(c == 0, A2, c))
                h = ((v * v >> 5) + (2 * m + 1) * v + 811 * d) & (V - 1)
                p = X[q][gr, h]; c = np.where(c == 0, p, c)
            fa, fb, fab = [misfit(q, np.where(e == 0, c, e)) for e in (A2, B2, AB2)]
            count = np.add.reduce((fab > np.minimum(fa, fb)).reshape(8, L, M).astype(np.int64), axis=2)
            donor = p.reshape(8, L, M, 16)[:, :, 0]
            ga, la = np.nonzero((count <= E + (u & 1)) & first); ba = b[ga, la]
            new[r, ga, L * t + la] = AB[ga, la]; new[r, ga, ba] = donor[ga, la]
        X = new
    return {"y": np.ascontiguousarray(np.transpose(X, (0, 1, 3, 2))).reshape(N, 128, V).astype(BF)}

@@ -1,0 +1,709 @@
+from concourse.bass import DstId, RemoteDMATransfer
+from concourse.mybir import dt, AluOpType, AxisListType, ActivationFunctionType
+
+ALU = AluOpType
+ACT = ActivationFunctionType
+BF, F32, I32, U16 = "bfloat16", "float32", "int32", "uint16"
+KBIG = 2.0 ** 95
+ASC = 2.0 ** 50
+MAGIC = 1.5 * 2.0 ** 35
+KSUB = 2.0 ** 17
+TAU = 2.0 ** -71
+
+CFG = {"g0": "VAAA", "sq": "A", "first": "A", "rep": "A", "strict": True, "pes": True, "halves": [2, 2, 2, 2], "look": 0.0,
+       "start": [0, 0.3, 1.6, 4.5], "pace": [1, 1, 1.5, 1], "pr0": 1.1, "pq": 5.1, "pr": 6.1, "hb": [2, 2, 2, 2, 2, 2],
+       "yb": [0, 2, 6, 2], "after": [[0], [1], [2], [3]], "xs": [[0], [0], [0, 6, 7], [0, 6, 7]], "db": [1, 1, 1, 1],
+       "bonus": [0] * 11}
+CFG.update({'g0': 'AVAA', 'look': 300, 'frac': 0.5, 'gap': 1000, 'start': [0, 1.3, 2.6, 3.9], 'pace': [1, 1, 1, 1], 'pr0': 0.5, 'pq': 3.19, 'pr': 4.65,
+            'rings': {'Y': [0, 1], 'H': [4, 5], 'C': [2], 'X': [6, 7], 'D': [3]}, 'hc': 'A', 'last1': True,
+            'form': 'SYSY', 'te': 'V' * 20, 'int': False, 'bonus': [0] * 16})
+CFG.update({'start': [0, 0.58, 1.4, 2.1], 'pace': [0.97, 1, 1.04, 1], 'pr0': 0.5, 'pq': 2.55, 'pr': 3.37, 'hc': 'V', 'form': 'YYYY',
+            'bonus': [0, 0, 0, 0, 0, 724, 0, 0, 0, 7433, -16368, 3383, 0, 1423, 2441, 748],
+            'rings': {'Y': [0, 1], 'H': [4, 5, 7], 'C': [2], 'X': [6], 'D': [3]}})
+
+SCRATCH = {
+    "TA": ("sbuf", [128, 4096], BF), "TB": ("sbuf", [128, 4352], BF), "TC": ("sbuf", [128, 4352], BF),
+    "TD": ("sbuf", [128, 2048], BF), "TE": ("sbuf", [128, 2304], BF), "TF": ("sbuf", [128, 512], BF),
+    "AL2": ("sbuf", [128, 256], BF), "RES": ("sbuf", [128, 512], BF), "RESL": ("sbuf", [128, 512], BF),
+    "OFL": ("sbuf", [128, 16], U16),
+    "hwi": ("sbuf", [128, 4], I32), "gli": ("sbuf", [128, 4], I32), "mxb": ("sbuf", [128, 16], BF),
+    "P0": ("sbuf", [128, 24], F32), "P1": ("sbuf", [128, 24], F32), "P2": ("sbuf", [128, 24], F32), "P3": ("sbuf", [128, 24], F32),
+    "G4": ("sbuf", [128, 128], F32), "moff": ("sbuf", [128, 8], U16),
+    "ones": ("sbuf", [128, 1024], BF), "ones32": ("sbuf", [128, 128], F32),
+    "IB": ("sbuf", [128, 128], BF), "IK": ("sbuf", [128, 128], BF), "I32": ("sbuf", [128, 128], F32),
+    "BD0": ("sbuf", [128, 128], F32), "BD32": ("sbuf", [128, 128], F32), "BDB": ("sbuf", [128, 128], BF),
+    "SEL0": ("sbuf", [128, 32], BF), "SEL": ("sbuf", [128, 32], BF), "BC": ("sbuf", [128, 1024], BF),
+    "E16i": ("sbuf", [128, 256], I32), "E16": ("sbuf", [128, 256], F32),
+    "ci": ("sbuf", [128, 64], I32), "cf": ("sbuf", [128, 96], F32), "coff": ("sbuf", [128, 16], U16),
+    "UU": ("sbuf", [128, 4096], BF), "RT": ("sbuf", [128, 4096], BF), "A3": ("sbuf", [128, 768], BF), "IS": ("sbuf", [128, 128], BF),
+    "hc0": ("sbuf", [128, 128], F32), "half": ("sbuf", [128, 128], BF), "RD": ("sbuf", [128, 48], F32),
+    "WZ": ("sbuf", [128, 3 * 4 * 144], BF), "QB": ("sbuf", [128, 3 * 256], BF), "NT": ("sbuf", [128, 4], F32),
+    "A2": ("sbuf", [128, 768], BF), "H0": ("sbuf", [128, 768], U16), "pq": ("sbuf", [128, 3 * 384], F32), "pqi": ("sbuf", [128, 256], I32),
+    "lf": ("sbuf", [128, 3 * 256], F32), "li": ("sbuf", [128, 3 * 64], I32), "lu": ("sbuf", [128, 3 * 32], U16),
+    "km": ("sbuf", [128, 256], F32), "kb": ("sbuf", [128, 256], F32), "fa": ("sbuf", [128, 512], F32), "fb": ("sbuf", [128, 512], F32),
+    "ntm": ("sbuf", [128, 768], BF), "LB": ("sbuf", [128, 2 * 1792], BF), "MR": ("sbuf", [128, 2 * 3072], BF),
+    "tp": ("sbuf", [128, 20480], BF), "RR": ("sbuf", [128, 4096], BF), "pD": ("sbuf", [128, 1024], BF),
+    "off": ("sbuf", [128, 256], U16), "sf": ("sbuf", [128, 4 * 320], F32), "si": ("sbuf", [128, 4 * 128], I32),
+    "cE": ("sbuf", [128, 3 * 3072], BF), "aE": ("sbuf", [128, 4 * 512], F32),
+    "t1": ("sbuf", [128, 192], F32), "NW": ("sbuf", [128, 256], BF), "cnt": ("sbuf", [128, 32], BF),
+}
+for _b in range(8):
+    SCRATCH["PS%d" % _b] = ("psum", [128, 512], F32)
+
+LOCAL = ["lA", "lh", "lg", "lm", "lT0", "lT1", "y0", "y1", "y2", "y3"]
+ARRIVE = ["rA0", "rP1", "rP2", "rP3", "rB0", "rA1", "rA2", "rR0", "rB1", "rR1", "rS1", "rB2", "rE2", "rF2", "rOf", "rRes"]
+SEMAPHORES = ["cV", "cA", "cP", "cG", "sent"] + LOCAL + ARRIVE
+CSEM = {"V": "cV", "A": "cA", "P": "cP", "G": "cG"}
+
+CYC, PEC, HOP = 1.0, 0.5, 90.0
+CACHE = {}
+
+
+def build(g, core, T, topo):
+    k = T.rank_of(core)
+    nr = len(T.cores)
+    ops = []
+    tag = [10]
+    eng = {"V": g.vector, "A": g.scalar, "P": g.tensor, "G": g, "S": g.sync}
+
+    def ap(r):
+        st = r[3] if len(r) > 3 else 1
+        t = T[r[0]]
+        p = r[4] if len(r) > 4 else 128
+        return t[0:p, r[1]:r[2]] if st == 1 else t[0:p, r[1]:r[2]:st]
+
+    def cnt(r):
+        st = r[3] if len(r) > 3 else 1
+        return (r[2] - r[1] + st - 1) // st
+
+    def two(*rs):
+        return all(SCRATCH[r[0]][2] in (BF, U16) for r in rs)
+
+    def add(e, fn, rd, wr, cost, **kw):
+        d = {"e": e, "fn": fn, "rd": [r for r in rd if isinstance(r, tuple)], "wr": wr, "cost": cost, "tag": tag[0]}
+        d.update(kw)
+        ops.append(d)
+        return len(ops) - 1
+
+    def val(x):
+        return ap(x) if isinstance(x, tuple) else x
+
+    def vc(n):
+        return 50 + max(64, n) * CYC
+
+    def ts(out, a, s1, s2, o0, o1=None):
+        def fn():
+            if o1 is None:
+                return g.vector.tensor_scalar(ap(out), ap(a), val(s1), None, o0)
+            return g.vector.tensor_scalar(ap(out), ap(a), val(s1), val(s2), o0, o1)
+        add("V", fn, [a, s1, s2], [out], vc(cnt(a) * (0.5 if two(out, a) else 1)))
+
+    def tt(out, a, b, o):
+        ps = a[0].startswith("PS") or b[0].startswith("PS")
+        add("V", lambda: g.vector.tensor_tensor(ap(out), ap(a), ap(b), o), [a, b], [out],
+            vc(cnt(a) * (1 if ps else (1.5 if two(out, a, b) else 2))))
+
+    def cp(out, a):
+        add("V", lambda: g.vector.tensor_copy(ap(out), ap(a)), [a], [out], vc(cnt(a) * (0.5 if two(out, a) else 1)))
+
+    def ms(out, c):
+        add("V", lambda: g.vector.memset(ap(out), c), [], [out], vc(cnt(out) * 0.5))
+
+    def act(out, a, f, bias=0.0, scale=1.0, acc=None):
+        def fn():
+            if acc is None:
+                return g.scalar.activation(ap(out), ap(a), f, bias=val(bias), scale=val(scale))
+            return g.scalar.activation(ap(out), ap(a), f, bias=val(bias), scale=val(scale), accum_out=ap(acc))
+        add("A", fn, [a, bias, scale], [out] + ([acc] if acc else []), 20 + vc(cnt(a)))
+
+    def gat(e, out, win, off, b=None, o=None):
+        def fn():
+            w = ap(win).indirect(ap(off))
+            if e == "A":
+                return g.scalar.activation(ap(out), w, ACT.Copy)
+            if b is None:
+                return g.vector.tensor_copy(ap(out), w)
+            return g.vector.tensor_tensor(ap(out), w, ap(b), o)
+        add(e, fn, [win, off, b], [out], 55 + cnt(out) * 1.56 * CYC)
+
+    def sca(win, off, a, b=None):
+        def fn():
+            w = ap(win).indirect(ap(off))
+            if b is None:
+                return g.vector.tensor_copy(w, ap(a))
+            return g.vector.tensor_tensor(w, ap(a), ap(b), ALU.add)
+        add("V", fn, [off, a, b], [win], 55 + cnt(a) * 3.8 * CYC)
+
+    def mm(items):
+        def fn():
+            r = None
+            for (o, l, x, s0, s1) in items:
+                r = g.tensor.matmul(ap(o), ap(l), ap(x), s0, s1)
+            return r
+        c = sum((max(min(64, cnt(l)), cnt(x)) * (4 if SCRATCH[l[0]][2] == F32 else 1)) * PEC + 5 for (o, l, x, s0, s1) in items)
+        add("P", fn, [i[1] for i in items] + [i[2] for i in items], [i[0] for i in items], c)
+
+    def grp(items, start=True, stop=True):
+        n = len(items)
+        mm([(o, l, x, start and i == 0, stop and i == n - 1) for i, (o, l, x) in enumerate(items)])
+
+    def iota(out, pat, base, cm):
+        f = SCRATCH[out[0]][2] != I32
+        def fn():
+            if f:
+                return g.iota(ap(out), pat, base, cm, allow_small_or_imprecise_dtypes=True)
+            return g.iota(ap(out), pat, base, cm)
+        add("G", fn, [], [out], 130 + 2 * cnt(out) * CYC)
+
+    def sel(out, a, pat, o, base, cm):
+        add("G", lambda: g.affine_select(ap(out), ap(a), pat, o, 0.0, base, cm), [a], [out], 170 + 2 * cnt(out) * CYC)
+
+    def load(q, sem, out, src, lat):
+        add(q, lambda: eng[q].dma_start(ap(out), src()), [], [out], 60, sem=sem, lat=lat)
+
+    def store(q, sem, dst, a, lat):
+        add(q, lambda: eng[q].dma_start(dst(), ap(a)), [a], [], 60, sem=sem, lat=lat)
+
+    def send(parts, lat):
+        info = []
+        for i, (dk, src, dst, sem) in enumerate(parts):
+            to = T.cores[(k + dk) % nr]
+            es = topo.engines(core, to)
+            n = 1
+            while 2 * n * len(parts) <= len(es):
+                n *= 2
+            m = 0
+            for e_ in es[i * n:(i + 1) * n]:
+                m |= 1 << e_
+            info.append((to, m, n, src, dst, sem))
+
+        def fn():
+            if len(info) == 1:
+                to, m, n, src, dst, sem = info[0]
+                a_ = topo.addr(to)
+                return g.remote_dma(ap(dst), ap(src), T.sem[sem], T.sem.sent, a_[1], a_[0], m)
+            return g.remote_dma_fused([RemoteDMATransfer(dst_ids=[DstId(rid=topo.addr(to)[0], pnc=topo.addr(to)[1])], dma_engine_mask=m,
+                                                         remote_sem=T.sem[sem], src=ap(src), dst=ap(dst))
+                                       for (to, m, n, src, dst, sem) in info], local_sem=T.sem.sent)
+        s = add("G", fn, [p[1] for p in parts], [], 500, remote=sum(i[2] for i in info))
+        for (to, m, n, src, dst, sem) in info:
+            add("X", None, [], [dst], 0, sem=sem, n=n, lat=lat, after=s)
+
+    load("S", "lA", ("TA", 0, 256), lambda: T.ent[:, 0:256], 2000)
+    load("A", "lh", ("hwi", 0, 1), lambda: T.hw[:], 2000)
+    load("A", "lg", ("gli", 0, 1), lambda: T.goal[:], 2000)
+    load("A", "lm", ("mxb", 0, 16), lambda: T.mix[:], 2000)
+    load("S", "lT1", ("TA", 2048, 4096), lambda: T.ent[:, 2048:4096], 4000)
+    load("S", "lT0", ("TA", 256, 2048), lambda: T.ent[:, 256:2048], 6000)
+    send([(1, ("TA", 0, 256), ("TB", 0, 256), "rA0")], 3500)
+    ms(("P0", 2, 8), 0.0)
+    cp(("P0", 0, 1), ("hwi", 0, 1))
+    cp(("P0", 1, 2), ("gli", 0, 1))
+    cp(("P0", 8, 24), ("mxb", 0, 16))
+    send([(j, ("P0", 0, 24), ("P%d" % j, 0, 24), "rP%d" % j) for j in (1, 2, 3)], 3000)
+    send([(1, ("TA", 2048, 4096), ("TB", 2048, 4096), "rB0")], 8000)
+    send([(3, ("TA", 256, 512), ("TC", 256, 512), "rA1"), (2, ("TA", 512, 768), ("AL2", 0, 256), "rA2")], 9000)
+    send([(1, ("TA", 256, 2048), ("TB", 256, 2048), "rR0")], 15000)
+    store("S", "y0", lambda: T.y[:, 768:2048], ("TA", 768, 2048), 5000)
+
+    ms(("ones32", 0, 128), 1.0)
+    ms(("ones", 0, 1024), 1.0)
+    ms(("WZ", 0, 1728), 0.0)
+    ms(("hc0", 0, 64), -2047.5)
+    ms(("hc0", 64, 128), -2.0 ** 23)
+    ms(("half", 0, 128), -1.0 / 256)
+    ms(("RD", 0, 48), 0.0)
+    sel(("BD0", 0, 128), ("ones32", 0, 128), [[-16, 8], [0, 16]], ALU.is_ge, 0, 1)
+    sel(("BD32", 0, 128), ("BD0", 0, 128), [[16, 8], [0, 16]], ALU.is_ge, 15, -1)
+    sel(("G4", 0, 128), ("BD32", 0, 128), [[0, 8], [-1, 16]], ALU.is_ge, 3, 0)
+    sel(("I32", 0, 128), ("ones32", 0, 128), [[-1, 128]], ALU.is_equal, 0, 1)
+    iota(("ci", 48, 56), [[0, 8]], 0, 1)
+    ts(("ci", 56, 64), ("ci", 48, 56), 15, None, ALU.bitwise_and)
+    cp(("moff", 0, 8), ("ci", 56, 64))
+    iota(("ci", 0, 4), [[0, 4]], 0, 1)
+    iota(("cf", 0, 4), [[4, 4]], 0, 0)
+    iota(("ci", 16, 32), [[1, 16]], 0, 0)
+    iota(("ci", 32, 48), [[16, 16]], 0, 0)
+    iota(("E16i", 0, 256), [[0, 16], [-1, 16]], 16, 1)
+    sel(("SEL0", 0, 32), ("ones", 0, 32), [[-4, 32]], ALU.is_ge, 0, 1)
+    sel(("SEL", 0, 32), ("SEL0", 0, 32), [[4, 32]], ALU.is_ge, 3, -1)
+    sel(("BC", 0, 1024, 1, 64), ("ones", 0, 1024, 1, 64), [[-8, 8], [-1, 8], [0, 16]], ALU.is_equal, 0, 1)
+    GM = ("BD32", 0, 128, 16)
+    act(("IB", 0, 128), ("I32", 0, 128), ACT.Copy)
+    act(("IK", 0, 128), ("I32", 0, 128), ACT.Copy, scale=-KBIG)
+    act(("IS", 0, 128), ("I32", 0, 128), ACT.Copy, scale=KSUB)
+    act(("BDB", 0, 128), ("BD32", 0, 128), ACT.Copy)
+    ts(("ci", 4, 8), ("ci", 0, 4), 3, None, ALU.bitwise_and)
+    ts(("ci", 8, 12), ("ci", 0, 4), 15, None, ALU.bitwise_and)
+    tt(("cf", 4, 8), ("cf", 0, 4), ("ci", 4, 8), ALU.add)
+    ts(("cf", 8, 12), ("cf", 4, 8), 2.0, 1.0, ALU.mult, ALU.add)
+    ts(("cf", 12, 16), ("cf", 8, 12), 16.0, 2047.5, ALU.mult, ALU.add)
+    tt(("cf", 16, 20), ("cf", 8, 12), ("cf", 8, 12), ALU.mult)
+    for d in range(5):
+        ts(("cf", 20 + 4 * d, 24 + 4 * d), ("cf", 16, 20), -8.0, 811.0 * d + 8192 - 13.0 / 32, ALU.mult, ALU.add)
+    cp(("cf", 40, 41), ("ci", 8, 9))
+    ts(("cf", 48, 64), ("ci", 32, 48), ("cf", 40, 41), None, ALU.add)
+    ts(("cf", 64, 80), ("cf", 48, 64), 2048.0, None, ALU.add)
+    ms(("cf", 44, 45), 592.0 + 2047.5)
+    ms(("cf", 45, 46), 128.0)
+    ms(("cf", 46, 47), 1.0)
+    cp(("coff", 0, 16), ("ci", 16, 32))
+    ts(("E16i", 0, 256), ("E16i", 0, 256), 15, None, ALU.bitwise_and)
+    ts(("E16", 0, 256), ("E16i", 0, 256), 0.0, None, ALU.is_equal)
+    cp(("RD", 0, 16, 2), GM)
+    cp(("RD", 1, 16, 2), GM)
+    ts(("RD", 16, 32, 2), GM, -1.0, None, ALU.mult)
+    ts(("RD", 33, 48, 2), GM, -1.0, None, ALU.mult)
+    ms(("TB", 4096, 4352), 0.0)
+    ms(("TC", 4096, 4352), 0.0)
+    ms(("TE", 2048, 2304), 0.0)
+
+    PQ = ["P0", "P1", "P3"]
+    PR = ["P1", "P3", "P2"]
+    TQ = ["TA", "TB", "TC"]
+    AT = [("TB", 0), ("TC", 256), ("AL2", 0)]
+    BT = [("TB", 2048), ("TC", 2048), ("TD", 0)]
+
+    def square(out, a, bias, tmp):
+        if CFG["sq"] == "A":
+            act(out, a, ACT.Square, bias=bias)
+        else:
+            ts(tmp, a, bias, None, ALU.add)
+            tt(out, tmp, tmp, ALU.mult)
+
+    def fold(raw, kk, u):
+        ts(kk, raw, MAGIC, -MAGIC, ALU.add, ALU.add)
+        tt(u, raw, kk, ALU.subtract)
+
+    def place(u, bias, c, s, tmp, gi, hi, mask, out):
+        square(s, u, bias, tmp)
+        ts(gi, s, 1.0 / 32, c, ALU.mult, ALU.add)
+        ts(hi, gi, mask, None, ALU.bitwise_and)
+        cp(out, hi)
+
+    def wz(t, which, s):
+        b = (4 * t + which) * 144
+        return ("WZ", b + 15 - s, b + 143 - s)
+
+    def prep_q(t, XB):
+        p = PQ[t]
+        an, a0 = AT[t]
+        b = 4 * t * 144
+        ts(("WZ", b + 288 + 15, b + 288 + 143), ("G4", 0, 128), (p, 0, 1), None, ALU.mult)
+        ts(("WZ", b + 15, b + 143, 16), GM, (p, 0, 1), None, ALU.mult)
+        ts(("WZ", b + 144 + 15, b + 144 + 143, 16), GM, (p, 0, 1), 1.0 / ASC, ALU.mult, ALU.mult)
+        grp([((XB, 0, 64), ("I32", 0, 128), ("hc0", 0, 64))] +
+            [((XB, 0, 64), wz(t, 2, 4 * r), (an, a0 + r, a0 + 256, 4)) for r in range(4)])
+        q = 384 * t
+        fold((XB, 0, 64), ("pq", q, q + 64), ("pq", q + 64, q + 128))
+        for kap in range(4):
+            j = kap % 2
+            place(("pq", q + 64, q + 128), ("cf", 12 + kap, 13 + kap), ("cf", 20 + kap, 21 + kap), ("pq", q + 128 + 64 * j, q + 192 + 64 * j),
+                  ("pq", q + 256 + 64 * j, q + 320 + 64 * j), ("pqi", 128 * j, 128 * j + 64), ("pqi", 128 * j + 64, 128 * j + 128), 4095,
+                  ("H0", 256 * t + 64 * kap, 256 * t + 64 * kap + 64))
+        if "Y" in CFG["form"]:
+            ts(("A2", 256 * t, 256 * t + 256), (an, a0, a0 + 256), ASC, 512.0, ALU.mult, ALU.max)
+        if "S" in CFG["form"]:
+            ts(("A3", 256 * t, 256 * t + 256), (an, a0, a0 + 256), TAU, None, ALU.mult)
+        gat("V", ("QB", 256 * t, 256 * t + 128), (p, 8, 24), ("moff", 0, 8), ("BD32", 0, 128), ALU.mult)
+        ts(("NT", t, t + 1), (p, 1, 2), -1.0, None, ALU.mult)
+
+    def prep_r(t, DB):
+        p = PR[t]
+        an, a0 = AT[t]
+        b = (4 * t + 3) * 144
+        ts(("WZ", b + 15, b + 143, 16), GM, (p, 0, 1), None, ALU.mult)
+        grp([((DB, 0, 16), ("I32", 0, 128), ("hc0", 0, 16))] +
+            [((DB, 0, 16), wz(t, 3, s), (an, a0 + s, a0 + 256, 16)) for s in range(16)])
+
+        def lf(j):
+            return ("lf", 256 * t + 16 * j, 256 * t + 16 * j + 16)
+
+        def li(j):
+            return ("li", 64 * t + 16 * j, 64 * t + 16 * j + 16)
+        boff, soff = ("lu", 32 * t, 32 * t + 16), ("lu", 32 * t + 16, 32 * t + 32)
+        fold((DB, 0, 16), lf(0), lf(1))
+        place(lf(1), ("cf", 44, 45), 16384.0 - 10952 - 13.0 / 32, lf(2), lf(3), li(0), li(1), 2047, boff)
+        ts(lf(4), li(1), 512.0, None, ALU.mult)
+        tt(lf(6), lf(4), ("cf", 48, 64), ALU.add)
+        ts(lf(5), lf(6), -1.0, 128.5, ALU.mult, ALU.add)
+        gat("V", ("km", 0, 256), lf(6), ("coff", 0, 16), ("E16", 0, 256), ALU.mult)
+        grp([((DB, 0, 256), ("BD32", 0, 128), ("km", 0, 256))])
+        act(("kb", 0, 256), (DB, 0, 256), ACT.Copy)
+        for c in range(16):
+            n, o = 16 * (c + 1), 256 * (c % 2)
+            col = 256 * t + 80 + c
+            act(("fa", o, o + n), ("kb", 0, n), ACT.Abs, bias=("lf", col, col + 1))
+            res = ("lf", col + 32, col + 33)
+            if CFG["first"] == "A":
+                act(("fb", o, o + n), ("fa", o, o + n), ACT.Relu, bias=("cf", 45, 46), scale=-1.0, acc=res)
+            else:
+                def fn(res=res, o=o, n=n):
+                    return g.vector.tensor_reduce(ap(res), ap(("fa", o, o + n)), AxisListType.X, ALU.min)
+                add("V", fn, [("fa", o, o + n)], [res], vc(n))
+        if CFG["first"] == "A":
+            ts(lf(8), lf(7), 0.25, None, ALU.is_gt)
+        else:
+            ts(lf(8), lf(7), 128.0, None, ALU.is_lt)
+        ts(li(2), lf(1), 2047.5, None, ALU.add)
+        ts(li(3), li(2), 1, None, ALU.bitwise_and)
+        ts(lf(9), lf(8), -32.0, -5.5, ALU.mult, ALU.add)
+        tt(lf(10), lf(9), li(3), ALU.add)
+        gat("V", ("ntm", 256 * t, 256 * t + 256), lf(10), ("coff", 0, 16), ("E16", 0, 256), ALU.mult)
+        tt(lf(11), lf(8), ("cf", 64, 80), ALU.mult)
+        tt(lf(12), lf(11), li(1), ALU.max)
+        cp(soff, lf(12))
+        if t == 2:
+            send([(-2, soff, ("OFL", 0, 16), "rOf")], 3000)
+
+    def prep_b(t):
+        an, a0 = AT[t]
+        bn, b0 = BT[t]
+        boff = ("lu", 32 * t, 32 * t + 16)
+        gat("A", lb(t, 0), (bn, b0, b0 + 2048), boff)
+        ts(lb(t, 1), (an, a0, a0 + 256), 0.0, None, ALU.is_equal)
+        tt(lb(t, 2), lb(t, 1), lb(t, 0), ALU.mult)
+        tt(lb(t, 3), lb(t, 2), (an, a0, a0 + 256), ALU.add)
+        for e, src in enumerate([lb(t, 3), (an, a0, a0 + 256), lb(t, 0)]):
+            o = 3072 * (t % 2) + 1024 * e
+            for j in range(4):
+                if CFG["rep"] == "A":
+                    act(("MR", o + j, o + 1024, 4), src, ACT.Relu, bias=("cf", 46, 47), scale=-1.0)
+                else:
+                    ts(("MR", o + j, o + 1024, 4), src, 0.0, None, ALU.is_equal)
+
+    def lb(t, j):
+        o = 1792 * (t % 2) + 256 * j
+        return ("LB", o, o + 256)
+
+    turn = {}
+
+    def bank(kind):
+        r = CFG["rings"][kind]
+        turn[kind] = turn.get(kind, -1) + 1
+        return "PS%d" % r[turn[kind] % len(r)]
+
+    def step(t, kap, d):
+        sl = kap
+        o = 1024 * sl
+        ot = 5120 * sl + 1024 * d
+        win = (TQ[t], 0, 4096)
+        nh = CFG["halves"][kap]
+        w = 1024 // nh
+        sub = CFG["form"][kap] == "S"
+
+        def sf(j):
+            return ("sf", 320 * sl + 64 * j, 320 * sl + 64 * j + 64)
+        for h in range(nh):
+            tp, rr = ("tp", ot + w * h, ot + w * h + w), ("RR", o + w * h, o + w * h + w)
+            f = w // 16
+            off = ("off", 64 * sl + f * h, 64 * sl + f * h + f)
+            to, how = (("UU", o + w * h, o + w * h + w), ALU.subtract) if sub else (tp, ALU.min)
+            if d == 0:
+                b = 256 * t + 64 * kap + f * h
+                gat(CFG["g0"][kap], tp, win, ("H0", b, b + f))
+                continue
+            if d == 4 and kap == 0:
+                gat("A", ("pD", w * h, w * h + w), win, off)
+                tt(to, ("pD", w * h, w * h + w), rr, how)
+            else:
+                gat("V", to, win, off, rr, how)
+            if sub:
+                if d < 4:
+                    act(rr, to, ACT.Abs, scale=KSUB)
+                if CFG["te"][5 * kap + d] == "A":
+                    act(tp, to, ACT.Relu)
+                else:
+                    ts(tp, to, 0.0, None, ALU.max)
+        if d == 4:
+            return
+        for h in range(2):
+            rr = ("RR", o + 512 * h, o + 512 * h + 512)
+            if d == 0 or not sub:
+                yb = bank("Y")
+                it = [((yb, 0, 512), ("IS" if sub else "IK", 0, 128), ("tp", ot + 512 * h, ot + 512 * h + 512))]
+                if d == 0:
+                    an, a = ("A3" if sub else "A2"), 256 * t + 128 * h
+                    it += [((yb, j, 512, 4), ("IB", 0, 128), (an, a, a + 128)) for j in range(4)]
+                else:
+                    it = [((yb, 0, 512), ("IB", 0, 128), rr)] + it
+                grp(it)
+                act(rr, (yb, 0, 512), ACT.Relu)
+            if sub:
+                ts(("RT", o + 512 * h, o + 512 * h + 512), rr, 1.0 / (TAU * KSUB ** d), 4096.0, ALU.mult, ALU.min)
+        whole = sub or CFG["int"]
+        first = ("hc0", 64, 128) if whole else ("hc0", 0, 64)
+        hp = (bank("H"), 0, 64)
+        old, new = first if d == 0 else sf(4 * (d % 2)), sf(4 * ((d + 1) % 2))
+        it = [(hp, wz(t, 0, s), ("tp", ot + s, ot + 1024, 16)) for s in range(16)]
+        hr = [(wz(t, 0, s), ("RT", o + s, o + 1024, 16)) if sub else (wz(t, 1, s), ("RR", o + s, o + 1024, 16)) for s in range(16)]
+        si = [("si", 128 * sl, 128 * sl + 64), ("si", 128 * sl + 64, 128 * sl + 128)]
+        if d == 3 and CFG["last1"] and not whole:
+            grp([(hp, ("I32", 0, 128), old)] + it, stop=False)
+            grp([(hp,) + hr[s] for s in range(16)], start=False)
+        else:
+            if CFG["hc"] == "A" and d == 0:
+                grp(it)
+                act(new, hp, ACT.Identity, bias=(first[0], first[1], first[1] + 1))
+            elif CFG["hc"] == "A":
+                grp([(hp, ("I32", 0, 128), old)] + it)
+                act(new, hp, ACT.Copy)
+            else:
+                grp(it)
+                tt(new, hp, old, ALU.add)
+            hp = (bank("H"), 0, 64)
+            grp(([] if whole else [(hp, ("I32", 0, 128), new)]) + [(hp,) + hr[s] for s in range(16)])
+        if whole:
+            tt(si[0], hp, new, ALU.add)
+            ts(si[1], si[0], 4095, None, ALU.bitwise_and)
+            ts(sf(2), si[1], -2047.5, None, ALU.add)
+        else:
+            fold(hp, sf(1), sf(2))
+        c = 24 + 4 * d + kap
+        place(sf(2), ("cf", 12 + kap, 13 + kap), ("cf", c, c + 1), sf(3), sf(1), si[0], si[1], 4095, ("off", 64 * sl, 64 * sl + 64))
+
+    def masks(t, kap):
+        sl = kap % 3
+        for h in range(2):
+            yb = bank("C")
+            for d0, d1 in ((0, 2), (2, 4), (4, 5)):
+                grp([((yb, 0, 512), ("IB", 0, 128), ("tp", 5120 * kap + 1024 * d + 512 * h, 5120 * kap + 1024 * d + 512 * h + 512))
+                     for d in range(d0, d1)], start=(d0 == 0), stop=(d1 == 5))
+            for e in range(3):
+                o, mo = 3072 * sl + 1024 * e + 512 * h, 3072 * (t % 2) + 1024 * e + 512 * h
+                tt(("cE", o, o + 512), (yb, 0, 512), ("MR", mo, mo + 512), ALU.mult)
+
+    ring = [0]
+
+    def verdict(t, kap):
+        sl = kap % 3
+        an, a0 = AT[t]
+        DB = bank("D")
+        mm([((DB, 0, 128), ("ones", 0, 128), ("half", 0, 128), True, False)])
+        srcs = [lb(t, 3)[:2], (an, a0), lb(t, 0)[:2]]
+        for h in range(2):
+            for e in range(3):
+                xb = bank("X")
+                ae = 512 * (ring[0] % 4)
+                ring[0] += 1
+                o = 3072 * sl + 1024 * e + 512 * h
+                sn, s0 = srcs[e]
+                grp([((xb, 0, 512), ("QB", 256 * t, 256 * t + 128), ("cE", o, o + 512))], stop=False)
+                grp([((xb, j, 512, 4), ("QB", 256 * t, 256 * t + 128), (sn, s0 + 128 * h, s0 + 128 * h + 128)) for j in range(4)], start=False)
+                act(("aE", ae, ae + 512), (xb, 0, 512), ACT.Abs, bias=("NT", t, t + 1))
+                for b0 in (0, 2):
+                    mm([((DB, 64 * h + 16 * b, 64 * h + 16 * b + 16), ("aE", ae + 128 * b, ae + 128 * b + 128), ("RD", 16 * e, 16 * e + 16),
+                         False, h == 1 and e == 2 and b == 3) for b in (b0, b0 + 1)])
+        t1 = ("t1", 64 * sl, 64 * sl + 64)
+        ts(t1, (DB, 0, 128, 2), -2.0 ** 22, 0.0, ALU.mult, ALU.min)
+        tt(("NW", 64 * kap, 64 * kap + 64), (DB, 1, 128, 2), t1, ALU.is_lt)
+
+    def tail(t):
+        an, a0 = AT[t]
+        mm([(("PS5", 0, 256), ("BDB", 0, 128), ("ntm", 256 * t, 256 * t + 256), True, False)])
+        grp([(("PS4", 0, 32, 1, 64), ("NW", 64 * j, 64 * j + 64), ("SEL", 0, 32)) for j in range(4)])
+        act(("cnt", 0, 32, 1, 64), ("PS4", 0, 32, 1, 64), ACT.Copy)
+        grp([(("PS5", 32 * j, 32 * j + 32), ("BC", 128 * j, 128 * j + 128, 1, 64), ("cnt", 0, 32, 1, 64)) for j in range(8)], start=False)
+        ts(lb(t, 5), ("PS5", 0, 256), 0.0, None, ALU.is_gt)
+        tt(lb(t, 6), lb(t, 5), lb(t, 4), ALU.mult)
+        if t < 2:
+            sca((BT[t][0], 2048, 4352), ("lu", 32 * t + 16, 32 * t + 32), lb(t, 6), lb(t, 0))
+        else:
+            tt(("RES", 256, 512), lb(t, 6), lb(t, 0), ALU.add)
+        tt(lb(t, 1), lb(t, 5), lb(t, 2), ALU.mult)
+        tt((an, a0, a0 + 256) if t < 2 else ("RES", 0, 256), lb(t, 1), (an, a0, a0 + 256), ALU.add)
+
+    prep_q(0, "PS5")
+    for t in range(3):
+        if t == 1:
+            send([(2, ("TB", 2048, 4096), ("TC", 2048, 4096), "rB1")], 8000)
+            send([(2, ("TB", 512, 2048), ("TC", 512, 2048), "rR1")], 14000)
+            send([(2, ("TB", 0, 256), ("TC", 0, 256), "rS1")], 15000)
+        if t == 2:
+            send([(-1, ("TC", 2048, 4096), ("TD", 0, 2048), "rB2")], 8000)
+            send([(1, ("TC", 2048, 4096), ("TE", 0, 2048), "rE2")], 15000)
+            send([(1, ("TC", 0, 512), ("TF", 0, 512), "rF2")], 17000)
+            store("S", "y1", lambda: T.y[:, 0:512], ("TF", 0, 512), 3000)
+        units = [(CFG["start"][kap] + d * CFG["pace"][kap], kap, d) for kap in range(4) for d in range(5)]
+        if t == 0:
+            units.append((CFG["pr0"], 4, 0))
+        if t < 2:
+            units += [(CFG["pq"], 5, 0), (CFG["pr"], 4, t + 1)]
+        for (_, kap, d) in sorted(units):
+            tag[0] = kap
+            if kap == 4:
+                prep_r(d, bank("H"))
+            elif kap == 5:
+                prep_q(t + 1, bank("H"))
+            else:
+                step(t, kap, d)
+            if d < 4 or kap > 3:
+                continue
+            if kap == 0:
+                tag[0] = 11
+                prep_b(t)
+                tt(lb(t, 4), ("pD", 0, 1024, 4), lb(t, 0), ALU.subtract)
+            tag[0] = 12 + kap
+            masks(t, kap)
+            tag[0] = 6 + kap
+            verdict(t, kap)
+        tag[0] = 10
+        tail(t)
+    send([(-2, ("RES", 0, 512), ("RESL", 0, 512), "rRes")], 4000)
+    sca(("TE", 0, 2304), ("OFL", 0, 16), ("RESL", 256, 512))
+    store("S", "y2", lambda: T.y[:, 2048:4096], ("TE", 0, 2048), 4500)
+    store("A", "y3", lambda: T.y[:, 512:768], ("RESL", 0, 256), 2500)
+    return ops, eng
+
+
+def depend(ops):
+    n = len(ops)
+    deps = [dict() for _ in range(n)]
+    hist = {}
+    for i, o in enumerate(ops):
+        acc = [(r, False) for r in o["rd"]] + [(r, True) for r in o["wr"]]
+        for r, w in acc:
+            ps = r[0].startswith("PS")
+            for (j, lo, hi, w2, st) in hist.get(r[0], []):
+                if j == i:
+                    continue
+                same = ops[j]["e"] == o["e"] and "sem" not in ops[j] and "remote" not in ops[j] and "sem" not in o and "remote" not in o
+                over = lo < r[2] and r[1] < hi
+                if same and len(r) > 3 and st == r[3] and (lo - r[1]) % st:
+                    over = False
+                if ps and not same:
+                    deps[i][j] = True
+                elif ps:
+                    deps[i].setdefault(j, False)
+                elif over and (w or w2):
+                    if (not same) or (w2 and not w) or CFG.get("strict"):
+                        deps[i][j] = True
+                    else:
+                        deps[i].setdefault(j, False)
+        for r, w in acc:
+            h = hist.setdefault(r[0], [])
+            if r[0].startswith("PS"):
+                h[:] = []
+            elif w and len(r) <= 3:
+                h[:] = [x for x in h if not (r[1] <= x[1] and x[2] <= r[2]) or x[0] == i]
+            h.append((i, r[1], r[2], w, r[3] if len(r) > 3 else 1))
+        if "after" in o:
+            deps[i][o["after"]] = False
+    last = None
+    for i, o in enumerate(ops):
+        if "remote" in o:
+            if last is not None:
+                deps[i].setdefault(last, False)
+            last = i
+    return deps
+
+
+def plan(ops, deps=None):
+    n = len(ops)
+    if deps is None:
+        deps = depend(ops)
+    succ = [[] for _ in range(n)]
+    for i in range(n):
+        for j in deps[i]:
+            succ[j].append(i)
+    full = [o["cost"] + o.get("lat", 0) for o in ops]
+    pri = [0.0] * n
+    for i in range(n - 1, -1, -1):
+        pri[i] = full[i] + max([pri[s] + (HOP if deps[s][i] else 0) for s in succ[i]] + [0.0])
+    left = [len(deps[i]) for i in range(n)]
+    ready = [0.0] * n
+    fin = [0.0] * n
+    free = {e: 0.0 for e in "VAPGSX"}
+    pool = {e: [] for e in "VAPGSX"}
+    for i in range(n):
+        if not left[i]:
+            pool[ops[i]["e"]].append(i)
+    order = []
+    look = CFG["look"]
+    rank = [pri[x] + CFG["bonus"][ops[x]["tag"]] for x in range(n)]
+    for _ in range(n):
+        best = None
+        for e in pool:
+            if pool[e]:
+                st = max(free[e], min(ready[i] for i in pool[e]))
+                if best is None or st < best[0]:
+                    best = (st, e)
+        st, e = best
+        i = max((x for x in pool[e] if ready[x] <= st), key=lambda x: (rank[x], -x))
+        soon = [x for x in pool[e] if st < ready[x] <= st + min(look, CFG["frac"] * ops[i]["cost"]) and rank[x] > rank[i] + CFG["gap"]]
+        if soon:
+            i = min(soon, key=lambda x: (ready[x], -rank[x]))
+        st = max(st, ready[i])
+        pool[e].remove(i)
+        free[e] = st + ops[i]["cost"]
+        fin[i] = st + full[i]
+        order.append(i)
+        for s in succ[i]:
+            ready[s] = max(ready[s], fin[i] + HOP if deps[s][i] or ops[s]["e"] == "X" else st + ops[i]["cost"])
+            left[s] -= 1
+            if not left[s]:
+                pool[ops[s]["e"]].append(s)
+    sig = [False] * n
+    known = {e: {} for e in "VAPGS"}
+    pos = {}
+    for p_, i in enumerate(order):
+        pos[i] = p_
+    clock = [None] * n
+    waits = [[] for _ in range(n)]
+    for i in order:
+        o = ops[i]
+        e = o["e"]
+        if e == "X":
+            clock[i] = {}
+            continue
+        kn = known[e]
+        need = sorted([j for j in deps[i] if deps[i][j]], key=lambda j: -pos[j])
+        for j in need:
+            key = ops[j].get("sem", ops[j]["e"])
+            if kn.get(key, -1) >= pos[j]:
+                continue
+            waits[i].append(j)
+            sig[j] = True
+            kn[key] = pos[j]
+            for a, b in clock[j].items():
+                if kn.get(a, -1) < b:
+                    kn[a] = b
+        clock[i] = dict(kn)
+    return order, waits, sig, max(fin), fin
+
+
+def rank_program(g, core, T, topo):
+    if T.rank_of(core) is None:
+        return
+    ops, eng = build(g, core, T, topo)
+    if "plan" not in CACHE:
+        CACHE["plan"] = plan(ops)
+    order, waits, sig = CACHE["plan"][:3]
+    count = {"V": 0, "A": 0, "P": 0, "G": 0}
+    mark = {}
+    sent = 0
+    for i in order:
+        o = ops[i]
+        e = o["e"]
+        if e == "X":
+            mark[i] = (o["sem"], o["n"])
+            continue
+        for j in waits[i]:
+            eng[e].wait_ge(T.sem[mark[j][0]], mark[j][1])
+        r = o["fn"]()
+        if "remote" in o:
+            sent += o["remote"]
+        elif "sem" in o:
+            r.then_inc(T.sem[o["sem"]], 16)
+            mark[i] = (o["sem"], 16)
+        elif sig[i]:
+            count[e] += 1
+            r.then_inc(T.sem[CSEM[e]], 1)
+            mark[i] = (CSEM[e], count[e])
+    for e in count:
+        if count[e]:
+            g.wait_ge(T.sem[CSEM[e]], count[e])
+    g.wait_ge(T.sem.sent, sent)
+    for i in order:
+        if "sem" in ops[i]:
+            g.wait_ge(T.sem[mark[i][0]], mark[i][1])

@@ -17,7 +17,7 @@ CFG = {"g0": "VAAA", "sq": "A", "first": "A", "rep": "A", "strict": True, "pes":
 CFG.update({'g0': 'AVAA', 'look': 300, 'frac': 0.5, 'gap': 1000, 'start': [0, 1.3, 2.6, 3.9], 'pace': [1, 1, 1, 1], 'pr0': 0.5, 'pq': 3.19, 'pr': 4.65,
             'rings': {'Y': [0, 1], 'H': [4, 5], 'C': [2], 'X': [6, 7], 'D': [3]}, 'hc': 'A', 'last1': True,
             'form': 'SYSY', 'te': 'V' * 20, 'int': False, 'bonus': [0] * 16})
-CFG.update({'start': [0, 0.58, 1.4, 2.1], 'pace': [0.97, 1, 1.04, 1], 'pr0': 0.5, 'pq': 2.55, 'pr': 3.37, 'hc': 'V', 'form': 'YYYY',
+CFG.update({'start': [0, 0.58, 1.4, 2.1], 'pace': [0.97, 1, 1.04, 1], 'pr0': 0.5, 'pq': 2.55, 'pr': 3.37, 'hc': 'V', 'form': 'YYYS', 'te': 'A' * 20, 'g0': 'AAAA', 'fa': 'VVVV', 'lin': 'A',
             'bonus': [0, 0, 0, 0, 0, 724, 0, 0, 0, 7433, -16368, 3383, 0, 1423, 2441, 748],
             'rings': {'Y': [0, 1], 'H': [4, 5, 7], 'C': [2], 'X': [6], 'D': [3]}})
 
@@ -50,12 +50,21 @@ SCRATCH = {
 for _b in range(8):
     SCRATCH["PS%d" % _b] = ("psum", [128, 512], F32)
 
-LOCAL = ["lA", "lh", "lg", "lm", "lT0", "lT1", "y0", "y1", "y2", "y3"]
+LOCAL = ["lA", "lh", "lg", "lm", "lT0", "lT1", "y0", "y1", "y2", "y3", "ac0", "ac1", "ac2", "ac3"]
 ARRIVE = ["rA0", "rP1", "rP2", "rP3", "rB0", "rA1", "rA2", "rR0", "rB1", "rR1", "rS1", "rB2", "rE2", "rF2", "rOf", "rRes"]
 SEMAPHORES = ["cV", "cA", "cP", "cG", "sent"] + LOCAL + ARRIVE
 CSEM = {"V": "cV", "A": "cA", "P": "cP", "G": "cG"}
 
-CYC, PEC, HOP = 1.0, 0.5, 90.0
+CFG.update({'g0': 'AVVA', 'halves': [2, 1, 2, 2], 'look': 200, 'start': [0, 0, 1.4, 2.32], 'pace': [0.71, 1.06, 1.01, 1.14], 'pr0': 0, 'pq': 2.75, 'pr': 2.69,
+            'bonus': [1001, 75, -1979, -3664, -1497, -732, 522, 524, -2905, 3915, -61723, 5433, 41454, 30119, 92, -3515], 'frac': 0.5, 'gap': 1000,
+            'rings': {'Y': [0, 2], 'H': [4, 5, 7], 'C': [2, 0], 'X': [6, 1], 'D': [3]}, 'hc': 'V', 'form': 'YYYY', 'te': 'V' * 20, 'fa': 'VVVV',
+            'acc': [3, 3, 3, 3]})
+CFG.update({'g0': 'VAAA', 'halves': [2, 2, 2, 2], 'look': 200, 'start': [0, 0.59, 1.4, 2.85], 'pace': [0.96, 1.07, 1.04, 1.31], 'pr0': 1.56, 'pq': 0.78, 'pr': 2.25,
+            'bonus': [1152, 0, 0, 0, 0, -4356, 18912, 3599, -183, 35417, -16368, 3778, 493, 2034, 2441, 11658], 'frac': 0.35, 'gap': 300,
+            'rings': {'Y': [0, 1, 2], 'H': [4, 5], 'C': [2, 0], 'X': [6, 7], 'D': [3]}, 'hc': 'A', 'last1': True, 'form': 'YYYS',
+            'te': 'V' * 20, 'int': False, 'fa': 'VVVV', 'lin': 'A', 'acc': [3, 3, 3, 3]})
+CYC, PEC, HOP = 0.9, 0.45, 110.0
+PAR = {"g": 1.56, "tt": 1.5, "fix": 50.0, "mm": 5.0, "af": 1.0}
 CACHE = {}
 
 
@@ -89,7 +98,7 @@ def build(g, core, T, topo):
         return ap(x) if isinstance(x, tuple) else x
 
     def vc(n):
-        return 50 + max(64, n) * CYC
+        return PAR["fix"] + max(64, n) * CYC
 
     def ts(out, a, s1, s2, o0, o1=None):
         def fn():
@@ -101,7 +110,7 @@ def build(g, core, T, topo):
     def tt(out, a, b, o):
         ps = a[0].startswith("PS") or b[0].startswith("PS")
         add("V", lambda: g.vector.tensor_tensor(ap(out), ap(a), ap(b), o), [a, b], [out],
-            vc(cnt(a) * (1 if ps else (1.5 if two(out, a, b) else 2))))
+            vc(cnt(a) * (1 if ps else (PAR["tt"] if two(out, a, b) else 2))))
 
     def cp(out, a):
         add("V", lambda: g.vector.tensor_copy(ap(out), ap(a)), [a], [out], vc(cnt(a) * (0.5 if two(out, a) else 1)))
@@ -124,7 +133,7 @@ def build(g, core, T, topo):
             if b is None:
                 return g.vector.tensor_copy(ap(out), w)
             return g.vector.tensor_tensor(ap(out), w, ap(b), o)
-        add(e, fn, [win, off, b], [out], 55 + cnt(out) * 1.56 * CYC)
+        add(e, fn, [win, off, b], [out], 55 + cnt(out) * PAR["g"] * CYC)
 
     def sca(win, off, a, b=None):
         def fn():
@@ -140,7 +149,7 @@ def build(g, core, T, topo):
             for (o, l, x, s0, s1) in items:
                 r = g.tensor.matmul(ap(o), ap(l), ap(x), s0, s1)
             return r
-        c = sum((max(min(64, cnt(l)), cnt(x)) * (4 if SCRATCH[l[0]][2] == F32 else 1)) * PEC + 5 for (o, l, x, s0, s1) in items)
+        c = sum((max(min(64, cnt(l)), cnt(x)) * (4 if SCRATCH[l[0]][2] == F32 else 1)) * PEC + PAR["mm"] for (o, l, x, s0, s1) in items)
         add("P", fn, [i[1] for i in items] + [i[2] for i in items], [i[0] for i in items], c)
 
     def grp(items, start=True, stop=True):
@@ -247,6 +256,9 @@ def build(g, core, T, topo):
     ms(("cf", 44, 45), 592.0 + 2047.5)
     ms(("cf", 45, 46), 128.0)
     ms(("cf", 46, 47), 1.0)
+    ms(("cf", 47, 48), 256.0)
+    ms(("cf", 80, 81), MAGIC)
+    ms(("cf", 81, 82), -MAGIC)
     cp(("coff", 0, 16), ("ci", 16, 32))
     ts(("E16i", 0, 256), ("E16i", 0, 256), 15, None, ALU.bitwise_and)
     ts(("E16", 0, 256), ("E16i", 0, 256), 0.0, None, ALU.is_equal)
@@ -271,8 +283,18 @@ def build(g, core, T, topo):
             ts(tmp, a, bias, None, ALU.add)
             tt(out, tmp, tmp, ALU.mult)
 
-    def fold(raw, kk, u):
-        ts(kk, raw, MAGIC, -MAGIC, ALU.add, ALU.add)
+    def lin(out, a, s):
+        if CFG["lin"] == "A":
+            act(out, a, ACT.Identity, scale=s)
+        else:
+            ts(out, a, s, None, ALU.mult)
+
+    def fold(raw, kk, u, e="V"):
+        if e == "A":
+            act(u, raw, ACT.Identity, bias=("cf", 80, 81))
+            act(kk, u, ACT.Identity, bias=("cf", 81, 82))
+        else:
+            ts(kk, raw, MAGIC, -MAGIC, ALU.add, ALU.add)
         tt(u, raw, kk, ALU.subtract)
 
     def place(u, bias, c, s, tmp, gi, hi, mask, out):
@@ -289,9 +311,9 @@ def build(g, core, T, topo):
         p = PQ[t]
         an, a0 = AT[t]
         b = 4 * t * 144
-        ts(("WZ", b + 288 + 15, b + 288 + 143), ("G4", 0, 128), (p, 0, 1), None, ALU.mult)
-        ts(("WZ", b + 15, b + 143, 16), GM, (p, 0, 1), None, ALU.mult)
-        ts(("WZ", b + 144 + 15, b + 144 + 143, 16), GM, (p, 0, 1), 1.0 / ASC, ALU.mult, ALU.mult)
+        lin(("WZ", b + 288 + 15, b + 288 + 143), ("G4", 0, 128), (p, 0, 1))
+        lin(("WZ", b + 15, b + 143, 16), GM, (p, 0, 1))
+        lin(("WZ", b + 144 + 15, b + 144 + 143, 16), ("WZ", b + 15, b + 143, 16), 1.0 / ASC)
         grp([((XB, 0, 64), ("I32", 0, 128), ("hc0", 0, 64))] +
             [((XB, 0, 64), wz(t, 2, 4 * r), (an, a0 + r, a0 + 256, 4)) for r in range(4)])
         q = 384 * t
@@ -304,15 +326,15 @@ def build(g, core, T, topo):
         if "Y" in CFG["form"]:
             ts(("A2", 256 * t, 256 * t + 256), (an, a0, a0 + 256), ASC, 512.0, ALU.mult, ALU.max)
         if "S" in CFG["form"]:
-            ts(("A3", 256 * t, 256 * t + 256), (an, a0, a0 + 256), TAU, None, ALU.mult)
+            ts(("A3", 256 * t, 256 * t + 256), (an, a0, a0 + 256), -256.0, -TAU, ALU.add, ALU.mult)
         gat("V", ("QB", 256 * t, 256 * t + 128), (p, 8, 24), ("moff", 0, 8), ("BD32", 0, 128), ALU.mult)
-        ts(("NT", t, t + 1), (p, 1, 2), -1.0, None, ALU.mult)
+        lin(("NT", t, t + 1), (p, 1, 2), -1.0)
 
     def prep_r(t, DB):
         p = PR[t]
         an, a0 = AT[t]
         b = (4 * t + 3) * 144
-        ts(("WZ", b + 15, b + 143, 16), GM, (p, 0, 1), None, ALU.mult)
+        lin(("WZ", b + 15, b + 143, 16), GM, (p, 0, 1))
         grp([((DB, 0, 16), ("I32", 0, 128), ("hc0", 0, 16))] +
             [((DB, 0, 16), wz(t, 3, s), (an, a0 + s, a0 + 256, 16)) for s in range(16)])
 
@@ -417,6 +439,9 @@ def build(g, core, T, topo):
                     ts(tp, to, 0.0, None, ALU.max)
         if d == 4:
             return
+        if 0 < d <= CFG["acc"][kap]:
+            c0, td = ("tp", 5120 * sl, 5120 * sl + 1024), ("tp", ot, ot + 1024)
+            add("G", lambda: g.dma_start(ap(c0), ap(td), accum_op=ALU.add), [td, c0], [c0], 1000, sem="ac%d" % kap, lat=3500)
         for h in range(2):
             rr = ("RR", o + 512 * h, o + 512 * h + 512)
             if d == 0 or not sub:
@@ -430,8 +455,8 @@ def build(g, core, T, topo):
                 grp(it)
                 act(rr, (yb, 0, 512), ACT.Relu)
             if sub:
-                ts(("RT", o + 512 * h, o + 512 * h + 512), rr, 1.0 / (TAU * KSUB ** d), 4096.0, ALU.mult, ALU.min)
-        whole = sub or CFG["int"]
+                act(("RT", o + 512 * h, o + 512 * h + 512), rr, ACT.Relu, bias=("cf", 47, 48), scale=-1.0 / (TAU * KSUB ** d))
+        whole = CFG["int"]
         first = ("hc0", 64, 128) if whole else ("hc0", 0, 64)
         hp = (bank("H"), 0, 64)
         old, new = first if d == 0 else sf(4 * (d % 2)), sf(4 * ((d + 1) % 2))
@@ -458,7 +483,7 @@ def build(g, core, T, topo):
             ts(si[1], si[0], 4095, None, ALU.bitwise_and)
             ts(sf(2), si[1], -2047.5, None, ALU.add)
         else:
-            fold(hp, sf(1), sf(2))
+            fold(hp, sf(1), sf(2), CFG["fa"][kap])
         c = 24 + 4 * d + kap
         place(sf(2), ("cf", 12 + kap, 13 + kap), ("cf", c, c + 1), sf(3), sf(1), si[0], si[1], 4095, ("off", 64 * sl, 64 * sl + 64))
 
@@ -466,9 +491,9 @@ def build(g, core, T, topo):
         sl = kap % 3
         for h in range(2):
             yb = bank("C")
-            for d0, d1 in ((0, 2), (2, 4), (4, 5)):
-                grp([((yb, 0, 512), ("IB", 0, 128), ("tp", 5120 * kap + 1024 * d + 512 * h, 5120 * kap + 1024 * d + 512 * h + 512))
-                     for d in range(d0, d1)], start=(d0 == 0), stop=(d1 == 5))
+            for d in [0] + list(range(CFG["acc"][kap] + 1, 5)):
+                grp([((yb, 0, 512), ("IB", 0, 128), ("tp", 5120 * kap + 1024 * d + 512 * h, 5120 * kap + 1024 * d + 512 * h + 512))],
+                    start=(d == 0), stop=(d == 4))
             for e in range(3):
                 o, mo = 3072 * sl + 1024 * e + 512 * h, 3072 * (t % 2) + 1024 * e + 512 * h
                 tt(("cE", o, o + 512), (yb, 0, 512), ("MR", mo, mo + 512), ALU.mult)
@@ -681,12 +706,14 @@ def rank_program(g, core, T, topo):
     order, waits, sig = CACHE["plan"][:3]
     count = {"V": 0, "A": 0, "P": 0, "G": 0}
     mark = {}
+    total = {}
     sent = 0
     for i in order:
         o = ops[i]
         e = o["e"]
         if e == "X":
             mark[i] = (o["sem"], o["n"])
+            total[o["sem"]] = o["n"]
             continue
         for j in waits[i]:
             eng[e].wait_ge(T.sem[mark[j][0]], mark[j][1])
@@ -695,7 +722,8 @@ def rank_program(g, core, T, topo):
             sent += o["remote"]
         elif "sem" in o:
             r.then_inc(T.sem[o["sem"]], 16)
-            mark[i] = (o["sem"], 16)
+            total[o["sem"]] = total.get(o["sem"], 0) + 16
+            mark[i] = (o["sem"], total[o["sem"]])
         elif sig[i]:
             count[e] += 1
             r.then_inc(T.sem[CSEM[e]], 1)
@@ -704,6 +732,5 @@ def rank_program(g, core, T, topo):
         if count[e]:
             g.wait_ge(T.sem[CSEM[e]], count[e])
     g.wait_ge(T.sem.sent, sent)
-    for i in order:
-        if "sem" in ops[i]:
-            g.wait_ge(T.sem[mark[i][0]], mark[i][1])
+    for s in total:
+        g.wait_ge(T.sem[s], total[s])

from concourse.bass import DstId, RemoteDMATransfer
from concourse.mybir import dt, AluOpType, AxisListType, ActivationFunctionType

ALU = AluOpType
ACT = ActivationFunctionType
BF, F32, I32, U16 = "bfloat16", "float32", "int32", "uint16"
KBIG = 2.0 ** 95
ASC = 2.0 ** 50
MAGIC = 1.5 * 2.0 ** 35
KSUB = 2.0 ** 17
TAU = 2.0 ** -71

CFG = {"g0": "VAAA", "sq": "A", "first": "A", "rep": "A", "strict": True, "pes": True, "halves": [2, 2, 2, 2], "look": 0.0,
       "start": [0, 0.3, 1.6, 4.5], "pace": [1, 1, 1.5, 1], "pr0": 1.1, "pq": 5.1, "pr": 6.1, "hb": [2, 2, 2, 2, 2, 2],
       "yb": [0, 2, 6, 2], "after": [[0], [1], [2], [3]], "xs": [[0], [0], [0, 6, 7], [0, 6, 7]], "db": [1, 1, 1, 1],
       "bonus": [0] * 11}
CFG.update({'g0': 'AVAA', 'look': 300, 'frac': 0.5, 'gap': 1000, 'start': [0, 1.3, 2.6, 3.9], 'pace': [1, 1, 1, 1], 'pr0': 0.5, 'pq': 3.19, 'pr': 4.65,
            'rings': {'Y': [0, 1], 'H': [4, 5], 'C': [2], 'X': [6, 7], 'D': [3]}, 'hc': 'A', 'last1': True,
            'form': 'SYSY', 'te': 'V' * 20, 'int': False, 'bonus': [0] * 16})
CFG.update({'start': [0, 0.58, 1.4, 2.1], 'pace': [0.97, 1, 1.04, 1], 'pr0': 0.5, 'pq': 2.55, 'pr': 3.37, 'hc': 'V', 'form': 'YYYS', 'te': 'A' * 20, 'g0': 'AAAA', 'fa': 'VVVV', 'lin': 'A',
            'bonus': [0, 0, 0, 0, 0, 724, 0, 0, 0, 7433, -16368, 3383, 0, 1423, 2441, 748],
            'rings': {'Y': [0, 1], 'H': [4, 5, 7], 'C': [2], 'X': [6], 'D': [3]}})

SCRATCH = {
    "TA": ("sbuf", [128, 4096], BF), "TB": ("sbuf", [128, 4352], BF), "TC": ("sbuf", [128, 4352], BF),
    "TD": ("sbuf", [128, 2048], BF), "TE": ("sbuf", [128, 2304], BF), "TF": ("sbuf", [128, 512], BF),
    "AL2": ("sbuf", [128, 256], BF), "RES": ("sbuf", [128, 512], BF), "RESL": ("sbuf", [128, 512], BF),
    "OFL": ("sbuf", [128, 16], U16),
    "hwi": ("sbuf", [128, 4], I32), "gli": ("sbuf", [128, 4], I32), "mxb": ("sbuf", [128, 16], BF),
    "P0": ("sbuf", [128, 24], F32), "P1": ("sbuf", [128, 24], F32), "P2": ("sbuf", [128, 24], F32), "P3": ("sbuf", [128, 24], F32),
    "G4": ("sbuf", [128, 128], F32), "moff": ("sbuf", [128, 8], U16),
    "ones": ("sbuf", [128, 1024], BF), "ones32": ("sbuf", [128, 128], F32),
    "IB": ("sbuf", [128, 128], BF), "IK": ("sbuf", [128, 128], BF), "I32": ("sbuf", [128, 128], F32),
    "BD0": ("sbuf", [128, 128], F32), "BD32": ("sbuf", [128, 128], F32), "BDB": ("sbuf", [128, 128], BF),
    "SEL0": ("sbuf", [128, 32], BF), "SEL": ("sbuf", [128, 32], BF), "BC": ("sbuf", [128, 1024], BF),
    "E16i": ("sbuf", [128, 256], I32), "E16": ("sbuf", [128, 256], F32),
    "ci": ("sbuf", [128, 64], I32), "cf": ("sbuf", [128, 96], F32), "coff": ("sbuf", [128, 16], U16),
    "UU": ("sbuf", [128, 4096], BF), "RT": ("sbuf", [128, 4096], BF), "A3": ("sbuf", [128, 768], BF), "IS": ("sbuf", [128, 128], BF),
    "hc0": ("sbuf", [128, 128], F32), "half": ("sbuf", [128, 128], BF), "RD": ("sbuf", [128, 48], F32),
    "WZ": ("sbuf", [128, 3 * 4 * 144], BF), "QB": ("sbuf", [128, 3 * 256], BF), "NT": ("sbuf", [128, 4], F32),
    "A2": ("sbuf", [128, 768], BF), "H0": ("sbuf", [128, 768], U16), "pq": ("sbuf", [128, 3 * 384], F32), "pqi": ("sbuf", [128, 256], I32),
    "lf": ("sbuf", [128, 3 * 256], F32), "li": ("sbuf", [128, 3 * 64], I32), "lu": ("sbuf", [128, 3 * 32], U16),
    "km": ("sbuf", [128, 256], F32), "kb": ("sbuf", [128, 256], F32), "fa": ("sbuf", [128, 512], F32), "fb": ("sbuf", [128, 512], F32),
    "ntm": ("sbuf", [128, 768], BF), "LB": ("sbuf", [128, 2 * 1792], BF), "MR": ("sbuf", [128, 2 * 3072], BF),
    "tp": ("sbuf", [128, 20480], BF), "RR": ("sbuf", [128, 4096], BF), "pD": ("sbuf", [128, 1024], BF),
    "off": ("sbuf", [128, 256], U16), "sf": ("sbuf", [128, 4 * 320], F32), "si": ("sbuf", [128, 4 * 128], I32),
    "cE": ("sbuf", [128, 3 * 3072], BF), "aE": ("sbuf", [128, 4 * 512], F32),
    "t1": ("sbuf", [128, 192], F32), "NW": ("sbuf", [128, 256], BF), "cnt": ("sbuf", [128, 32], BF),
}
for _b in range(8):
    SCRATCH["PS%d" % _b] = ("psum", [128, 512], F32)

LOCAL = ["lA", "lh", "lg", "lm", "lT0", "lT1", "y0", "y1", "y2", "y3", "ac0", "ac1", "ac2", "ac3"]
ARRIVE = ["rA0", "rP1", "rP2", "rP3", "rB0", "rA1", "rA2", "rR0", "rB1", "rR1", "rS1", "rB2", "rE2", "rF2", "rOf", "rRes"]
SEMAPHORES = ["cV", "cA", "cP", "cG", "sent"] + LOCAL + ARRIVE
CSEM = {"V": "cV", "A": "cA", "P": "cP", "G": "cG"}

CFG.update({'g0': 'AVVA', 'halves': [2, 1, 2, 2], 'look': 200, 'start': [0, 0, 1.4, 2.32], 'pace': [0.71, 1.06, 1.01, 1.14], 'pr0': 0, 'pq': 2.75, 'pr': 2.69,
            'bonus': [1001, 75, -1979, -3664, -1497, -732, 522, 524, -2905, 3915, -61723, 5433, 41454, 30119, 92, -3515], 'frac': 0.5, 'gap': 1000,
            'rings': {'Y': [0, 2], 'H': [4, 5, 7], 'C': [2, 0], 'X': [6, 1], 'D': [3]}, 'hc': 'V', 'form': 'YYYY', 'te': 'V' * 20, 'fa': 'VVVV',
            'acc': [3, 3, 3, 3]})
CFG.update({'g0': 'VAAA', 'halves': [2, 2, 2, 2], 'look': 200, 'start': [0, 0.59, 1.4, 2.85], 'pace': [0.96, 1.07, 1.04, 1.31], 'pr0': 1.56, 'pq': 0.78, 'pr': 2.25,
            'bonus': [1152, 0, 0, 0, 0, -4356, 18912, 3599, -183, 35417, -16368, 3778, 493, 2034, 2441, 11658], 'frac': 0.35, 'gap': 300,
            'rings': {'Y': [0, 1, 2], 'H': [4, 5], 'C': [2, 0], 'X': [6, 7], 'D': [3]}, 'hc': 'A', 'last1': True, 'form': 'YYYS',
            'te': 'V' * 20, 'int': False, 'fa': 'VVVV', 'lin': 'A', 'acc': [3, 3, 3, 3]})
CYC, PEC, HOP = 0.9, 0.45, 110.0
PAR = {"g": 1.56, "tt": 1.5, "fix": 50.0, "mm": 5.0, "af": 1.0}
CACHE = {}


def build(g, core, T, topo):
    k = T.rank_of(core)
    nr = len(T.cores)
    ops = []
    tag = [10]
    eng = {"V": g.vector, "A": g.scalar, "P": g.tensor, "G": g, "S": g.sync}

    def ap(r):
        st = r[3] if len(r) > 3 else 1
        t = T[r[0]]
        p = r[4] if len(r) > 4 else 128
        return t[0:p, r[1]:r[2]] if st == 1 else t[0:p, r[1]:r[2]:st]

    def cnt(r):
        st = r[3] if len(r) > 3 else 1
        return (r[2] - r[1] + st - 1) // st

    def two(*rs):
        return all(SCRATCH[r[0]][2] in (BF, U16) for r in rs)

    def add(e, fn, rd, wr, cost, **kw):
        d = {"e": e, "fn": fn, "rd": [r for r in rd if isinstance(r, tuple)], "wr": wr, "cost": cost, "tag": tag[0]}
        d.update(kw)
        ops.append(d)
        return len(ops) - 1

    def val(x):
        return ap(x) if isinstance(x, tuple) else x

    def vc(n):
        return PAR["fix"] + max(64, n) * CYC

    def ts(out, a, s1, s2, o0, o1=None):
        def fn():
            if o1 is None:
                return g.vector.tensor_scalar(ap(out), ap(a), val(s1), None, o0)
            return g.vector.tensor_scalar(ap(out), ap(a), val(s1), val(s2), o0, o1)
        add("V", fn, [a, s1, s2], [out], vc(cnt(a) * (0.5 if two(out, a) else 1)))

    def tt(out, a, b, o):
        ps = a[0].startswith("PS") or b[0].startswith("PS")
        add("V", lambda: g.vector.tensor_tensor(ap(out), ap(a), ap(b), o), [a, b], [out],
            vc(cnt(a) * (1 if ps else (PAR["tt"] if two(out, a, b) else 2))))

    def cp(out, a):
        add("V", lambda: g.vector.tensor_copy(ap(out), ap(a)), [a], [out], vc(cnt(a) * (0.5 if two(out, a) else 1)))

    def ms(out, c):
        add("V", lambda: g.vector.memset(ap(out), c), [], [out], vc(cnt(out) * 0.5))

    def act(out, a, f, bias=0.0, scale=1.0, acc=None):
        def fn():
            if acc is None:
                return g.scalar.activation(ap(out), ap(a), f, bias=val(bias), scale=val(scale))
            return g.scalar.activation(ap(out), ap(a), f, bias=val(bias), scale=val(scale), accum_out=ap(acc))
        add("A", fn, [a, bias, scale], [out] + ([acc] if acc else []), 20 + vc(cnt(a)))

    def gat(e, out, win, off, b=None, o=None):
        def fn():
            w = ap(win).indirect(ap(off))
            if e == "A":
                return g.scalar.activation(ap(out), w, ACT.Copy)
            if b is None:
                return g.vector.tensor_copy(ap(out), w)
            return g.vector.tensor_tensor(ap(out), w, ap(b), o)
        add(e, fn, [win, off, b], [out], 55 + cnt(out) * PAR["g"] * CYC)

    def sca(win, off, a, b=None):
        def fn():
            w = ap(win).indirect(ap(off))
            if b is None:
                return g.vector.tensor_copy(w, ap(a))
            return g.vector.tensor_tensor(w, ap(a), ap(b), ALU.add)
        add("V", fn, [off, a, b], [win], 55 + cnt(a) * 3.8 * CYC)

    def mm(items):
        def fn():
            r = None
            for (o, l, x, s0, s1) in items:
                r = g.tensor.matmul(ap(o), ap(l), ap(x), s0, s1)
            return r
        c = sum((max(min(64, cnt(l)), cnt(x)) * (4 if SCRATCH[l[0]][2] == F32 else 1)) * PEC + PAR["mm"] for (o, l, x, s0, s1) in items)
        add("P", fn, [i[1] for i in items] + [i[2] for i in items], [i[0] for i in items], c)

    def grp(items, start=True, stop=True):
        n = len(items)
        mm([(o, l, x, start and i == 0, stop and i == n - 1) for i, (o, l, x) in enumerate(items)])

    def iota(out, pat, base, cm):
        f = SCRATCH[out[0]][2] != I32
        def fn():
            if f:
                return g.iota(ap(out), pat, base, cm, allow_small_or_imprecise_dtypes=True)
            return g.iota(ap(out), pat, base, cm)
        add("G", fn, [], [out], 130 + 2 * cnt(out) * CYC)

    def sel(out, a, pat, o, base, cm):
        add("G", lambda: g.affine_select(ap(out), ap(a), pat, o, 0.0, base, cm), [a], [out], 170 + 2 * cnt(out) * CYC)

    def load(q, sem, out, src, lat):
        add(q, lambda: eng[q].dma_start(ap(out), src()), [], [out], 60, sem=sem, lat=lat)

    def store(q, sem, dst, a, lat):
        add(q, lambda: eng[q].dma_start(dst(), ap(a)), [a], [], 60, sem=sem, lat=lat)

    def send(parts, lat):
        info = []
        for i, (dk, src, dst, sem) in enumerate(parts):
            to = T.cores[(k + dk) % nr]
            es = topo.engines(core, to)
            n = 1
            while 2 * n * len(parts) <= len(es):
                n *= 2
            m = 0
            for e_ in es[i * n:(i + 1) * n]:
                m |= 1 << e_
            info.append((to, m, n, src, dst, sem))

        def fn():
            if len(info) == 1:
                to, m, n, src, dst, sem = info[0]
                a_ = topo.addr(to)
                return g.remote_dma(ap(dst), ap(src), T.sem[sem], T.sem.sent, a_[1], a_[0], m)
            return g.remote_dma_fused([RemoteDMATransfer(dst_ids=[DstId(rid=topo.addr(to)[0], pnc=topo.addr(to)[1])], dma_engine_mask=m,
                                                         remote_sem=T.sem[sem], src=ap(src), dst=ap(dst))
                                       for (to, m, n, src, dst, sem) in info], local_sem=T.sem.sent)
        s = add("G", fn, [p[1] for p in parts], [], 500, remote=sum(i[2] for i in info))
        for (to, m, n, src, dst, sem) in info:
            add("X", None, [], [dst], 0, sem=sem, n=n, lat=lat, after=s)

    load("S", "lA", ("TA", 0, 256), lambda: T.ent[:, 0:256], 2000)
    load("A", "lh", ("hwi", 0, 1), lambda: T.hw[:], 2000)
    load("A", "lg", ("gli", 0, 1), lambda: T.goal[:], 2000)
    load("A", "lm", ("mxb", 0, 16), lambda: T.mix[:], 2000)
    load("S", "lT1", ("TA", 2048, 4096), lambda: T.ent[:, 2048:4096], 4000)
    load("S", "lT0", ("TA", 256, 2048), lambda: T.ent[:, 256:2048], 6000)
    send([(1, ("TA", 0, 256), ("TB", 0, 256), "rA0")], 3500)
    ms(("P0", 2, 8), 0.0)
    cp(("P0", 0, 1), ("hwi", 0, 1))
    cp(("P0", 1, 2), ("gli", 0, 1))
    cp(("P0", 8, 24), ("mxb", 0, 16))
    send([(j, ("P0", 0, 24), ("P%d" % j, 0, 24), "rP%d" % j) for j in (1, 2, 3)], 3000)
    send([(1, ("TA", 2048, 4096), ("TB", 2048, 4096), "rB0")], 8000)
    send([(3, ("TA", 256, 512), ("TC", 256, 512), "rA1"), (2, ("TA", 512, 768), ("AL2", 0, 256), "rA2")], 9000)
    send([(1, ("TA", 256, 2048), ("TB", 256, 2048), "rR0")], 15000)
    store("S", "y0", lambda: T.y[:, 768:2048], ("TA", 768, 2048), 5000)

    ms(("ones32", 0, 128), 1.0)
    ms(("ones", 0, 1024), 1.0)
    ms(("WZ", 0, 1728), 0.0)
    ms(("hc0", 0, 64), -2047.5)
    ms(("hc0", 64, 128), -2.0 ** 23)
    ms(("half", 0, 128), -1.0 / 256)
    ms(("RD", 0, 48), 0.0)
    sel(("BD0", 0, 128), ("ones32", 0, 128), [[-16, 8], [0, 16]], ALU.is_ge, 0, 1)
    sel(("BD32", 0, 128), ("BD0", 0, 128), [[16, 8], [0, 16]], ALU.is_ge, 15, -1)
    sel(("G4", 0, 128), ("BD32", 0, 128), [[0, 8], [-1, 16]], ALU.is_ge, 3, 0)
    sel(("I32", 0, 128), ("ones32", 0, 128), [[-1, 128]], ALU.is_equal, 0, 1)
    iota(("ci", 48, 56), [[0, 8]], 0, 1)
    ts(("ci", 56, 64), ("ci", 48, 56), 15, None, ALU.bitwise_and)
    cp(("moff", 0, 8), ("ci", 56, 64))
    iota(("ci", 0, 4), [[0, 4]], 0, 1)
    iota(("cf", 0, 4), [[4, 4]], 0, 0)
    iota(("ci", 16, 32), [[1, 16]], 0, 0)
    iota(("ci", 32, 48), [[16, 16]], 0, 0)
    iota(("E16i", 0, 256), [[0, 16], [-1, 16]], 16, 1)
    sel(("SEL0", 0, 32), ("ones", 0, 32), [[-4, 32]], ALU.is_ge, 0, 1)
    sel(("SEL", 0, 32), ("SEL0", 0, 32), [[4, 32]], ALU.is_ge, 3, -1)
    sel(("BC", 0, 1024, 1, 64), ("ones", 0, 1024, 1, 64), [[-8, 8], [-1, 8], [0, 16]], ALU.is_equal, 0, 1)
    GM = ("BD32", 0, 128, 16)
    act(("IB", 0, 128), ("I32", 0, 128), ACT.Copy)
    act(("IK", 0, 128), ("I32", 0, 128), ACT.Copy, scale=-KBIG)
    act(("IS", 0, 128), ("I32", 0, 128), ACT.Copy, scale=KSUB)
    act(("BDB", 0, 128), ("BD32", 0, 128), ACT.Copy)
    ts(("ci", 4, 8), ("ci", 0, 4), 3, None, ALU.bitwise_and)
    ts(("ci", 8, 12), ("ci", 0, 4), 15, None, ALU.bitwise_and)
    tt(("cf", 4, 8), ("cf", 0, 4), ("ci", 4, 8), ALU.add)
    ts(("cf", 8, 12), ("cf", 4, 8), 2.0, 1.0, ALU.mult, ALU.add)
    ts(("cf", 12, 16), ("cf", 8, 12), 16.0, 2047.5, ALU.mult, ALU.add)
    tt(("cf", 16, 20), ("cf", 8, 12), ("cf", 8, 12), ALU.mult)
    for d in range(5):
        ts(("cf", 20 + 4 * d, 24 + 4 * d), ("cf", 16, 20), -8.0, 811.0 * d + 8192 - 13.0 / 32, ALU.mult, ALU.add)
    cp(("cf", 40, 41), ("ci", 8, 9))
    ts(("cf", 48, 64), ("ci", 32, 48), ("cf", 40, 41), None, ALU.add)
    ts(("cf", 64, 80), ("cf", 48, 64), 2048.0, None, ALU.add)
    ms(("cf", 44, 45), 592.0 + 2047.5)
    ms(("cf", 45, 46), 128.0)
    ms(("cf", 46, 47), 1.0)
    ms(("cf", 47, 48), 256.0)
    ms(("cf", 80, 81), MAGIC)
    ms(("cf", 81, 82), -MAGIC)
    cp(("coff", 0, 16), ("ci", 16, 32))
    ts(("E16i", 0, 256), ("E16i", 0, 256), 15, None, ALU.bitwise_and)
    ts(("E16", 0, 256), ("E16i", 0, 256), 0.0, None, ALU.is_equal)
    cp(("RD", 0, 16, 2), GM)
    cp(("RD", 1, 16, 2), GM)
    ts(("RD", 16, 32, 2), GM, -1.0, None, ALU.mult)
    ts(("RD", 33, 48, 2), GM, -1.0, None, ALU.mult)
    ms(("TB", 4096, 4352), 0.0)
    ms(("TC", 4096, 4352), 0.0)
    ms(("TE", 2048, 2304), 0.0)

    PQ = ["P0", "P1", "P3"]
    PR = ["P1", "P3", "P2"]
    TQ = ["TA", "TB", "TC"]
    AT = [("TB", 0), ("TC", 256), ("AL2", 0)]
    BT = [("TB", 2048), ("TC", 2048), ("TD", 0)]

    def square(out, a, bias, tmp):
        if CFG["sq"] == "A":
            act(out, a, ACT.Square, bias=bias)
        else:
            ts(tmp, a, bias, None, ALU.add)
            tt(out, tmp, tmp, ALU.mult)

    def lin(out, a, s):
        if CFG["lin"] == "A":
            act(out, a, ACT.Identity, scale=s)
        else:
            ts(out, a, s, None, ALU.mult)

    def fold(raw, kk, u, e="V"):
        if e == "A":
            act(u, raw, ACT.Identity, bias=("cf", 80, 81))
            act(kk, u, ACT.Identity, bias=("cf", 81, 82))
        else:
            ts(kk, raw, MAGIC, -MAGIC, ALU.add, ALU.add)
        tt(u, raw, kk, ALU.subtract)

    def place(u, bias, c, s, tmp, gi, hi, mask, out):
        square(s, u, bias, tmp)
        ts(gi, s, 1.0 / 32, c, ALU.mult, ALU.add)
        ts(hi, gi, mask, None, ALU.bitwise_and)
        cp(out, hi)

    def wz(t, which, s):
        b = (4 * t + which) * 144
        return ("WZ", b + 15 - s, b + 143 - s)

    def prep_q(t, XB):
        p = PQ[t]
        an, a0 = AT[t]
        b = 4 * t * 144
        lin(("WZ", b + 288 + 15, b + 288 + 143), ("G4", 0, 128), (p, 0, 1))
        lin(("WZ", b + 15, b + 143, 16), GM, (p, 0, 1))
        lin(("WZ", b + 144 + 15, b + 144 + 143, 16), ("WZ", b + 15, b + 143, 16), 1.0 / ASC)
        grp([((XB, 0, 64), ("I32", 0, 128), ("hc0", 0, 64))] +
            [((XB, 0, 64), wz(t, 2, 4 * r), (an, a0 + r, a0 + 256, 4)) for r in range(4)])
        q = 384 * t
        fold((XB, 0, 64), ("pq", q, q + 64), ("pq", q + 64, q + 128))
        for kap in range(4):
            j = kap % 2
            place(("pq", q + 64, q + 128), ("cf", 12 + kap, 13 + kap), ("cf", 20 + kap, 21 + kap), ("pq", q + 128 + 64 * j, q + 192 + 64 * j),
                  ("pq", q + 256 + 64 * j, q + 320 + 64 * j), ("pqi", 128 * j, 128 * j + 64), ("pqi", 128 * j + 64, 128 * j + 128), 4095,
                  ("H0", 256 * t + 64 * kap, 256 * t + 64 * kap + 64))
        if "Y" in CFG["form"]:
            ts(("A2", 256 * t, 256 * t + 256), (an, a0, a0 + 256), ASC, 512.0, ALU.mult, ALU.max)
        if "S" in CFG["form"]:
            ts(("A3", 256 * t, 256 * t + 256), (an, a0, a0 + 256), -256.0, -TAU, ALU.add, ALU.mult)
        gat("V", ("QB", 256 * t, 256 * t + 128), (p, 8, 24), ("moff", 0, 8), ("BD32", 0, 128), ALU.mult)
        lin(("NT", t, t + 1), (p, 1, 2), -1.0)

    def prep_r(t, DB):
        p = PR[t]
        an, a0 = AT[t]
        b = (4 * t + 3) * 144
        lin(("WZ", b + 15, b + 143, 16), GM, (p, 0, 1))
        grp([((DB, 0, 16), ("I32", 0, 128), ("hc0", 0, 16))] +
            [((DB, 0, 16), wz(t, 3, s), (an, a0 + s, a0 + 256, 16)) for s in range(16)])

        def lf(j):
            return ("lf", 256 * t + 16 * j, 256 * t + 16 * j + 16)

        def li(j):
            return ("li", 64 * t + 16 * j, 64 * t + 16 * j + 16)
        boff, soff = ("lu", 32 * t, 32 * t + 16), ("lu", 32 * t + 16, 32 * t + 32)
        fold((DB, 0, 16), lf(0), lf(1))
        place(lf(1), ("cf", 44, 45), 16384.0 - 10952 - 13.0 / 32, lf(2), lf(3), li(0), li(1), 2047, boff)
        ts(lf(4), li(1), 512.0, None, ALU.mult)
        tt(lf(6), lf(4), ("cf", 48, 64), ALU.add)
        ts(lf(5), lf(6), -1.0, 128.5, ALU.mult, ALU.add)
        gat("V", ("km", 0, 256), lf(6), ("coff", 0, 16), ("E16", 0, 256), ALU.mult)
        grp([((DB, 0, 256), ("BD32", 0, 128), ("km", 0, 256))])
        act(("kb", 0, 256), (DB, 0, 256), ACT.Copy)
        for c in range(16):
            n, o = 16 * (c + 1), 256 * (c % 2)
            col = 256 * t + 80 + c
            act(("fa", o, o + n), ("kb", 0, n), ACT.Abs, bias=("lf", col, col + 1))
            res = ("lf", col + 32, col + 33)
            if CFG["first"] == "A":
                act(("fb", o, o + n), ("fa", o, o + n), ACT.Relu, bias=("cf", 45, 46), scale=-1.0, acc=res)
            else:
                def fn(res=res, o=o, n=n):
                    return g.vector.tensor_reduce(ap(res), ap(("fa", o, o + n)), AxisListType.X, ALU.min)
                add("V", fn, [("fa", o, o + n)], [res], vc(n))
        if CFG["first"] == "A":
            ts(lf(8), lf(7), 0.25, None, ALU.is_gt)
        else:
            ts(lf(8), lf(7), 128.0, None, ALU.is_lt)
        ts(li(2), lf(1), 2047.5, None, ALU.add)
        ts(li(3), li(2), 1, None, ALU.bitwise_and)
        ts(lf(9), lf(8), -32.0, -5.5, ALU.mult, ALU.add)
        tt(lf(10), lf(9), li(3), ALU.add)
        gat("V", ("ntm", 256 * t, 256 * t + 256), lf(10), ("coff", 0, 16), ("E16", 0, 256), ALU.mult)
        tt(lf(11), lf(8), ("cf", 64, 80), ALU.mult)
        tt(lf(12), lf(11), li(1), ALU.max)
        cp(soff, lf(12))
        if t == 2:
            send([(-2, soff, ("OFL", 0, 16), "rOf")], 3000)

    def prep_b(t):
        an, a0 = AT[t]
        bn, b0 = BT[t]
        boff = ("lu", 32 * t, 32 * t + 16)
        gat("A", lb(t, 0), (bn, b0, b0 + 2048), boff)
        ts(lb(t, 1), (an, a0, a0 + 256), 0.0, None, ALU.is_equal)
        tt(lb(t, 2), lb(t, 1), lb(t, 0), ALU.mult)
        tt(lb(t, 3), lb(t, 2), (an, a0, a0 + 256), ALU.add)
        for e, src in enumerate([lb(t, 3), (an, a0, a0 + 256), lb(t, 0)]):
            o = 3072 * (t % 2) + 1024 * e
            for j in range(4):
                if CFG["rep"] == "A":
                    act(("MR", o + j, o + 1024, 4), src, ACT.Relu, bias=("cf", 46, 47), scale=-1.0)
                else:
                    ts(("MR", o + j, o + 1024, 4), src, 0.0, None, ALU.is_equal)

    def lb(t, j):
        o = 1792 * (t % 2) + 256 * j
        return ("LB", o, o + 256)

    turn = {}

    def bank(kind):
        r = CFG["rings"][kind]
        turn[kind] = turn.get(kind, -1) + 1
        return "PS%d" % r[turn[kind] % len(r)]

    def step(t, kap, d):
        sl = kap
        o = 1024 * sl
        ot = 5120 * sl + 1024 * d
        win = (TQ[t], 0, 4096)
        nh = CFG["halves"][kap]
        w = 1024 // nh
        sub = CFG["form"][kap] == "S"

        def sf(j):
            return ("sf", 320 * sl + 64 * j, 320 * sl + 64 * j + 64)
        for h in range(nh):
            tp, rr = ("tp", ot + w * h, ot + w * h + w), ("RR", o + w * h, o + w * h + w)
            f = w // 16
            off = ("off", 64 * sl + f * h, 64 * sl + f * h + f)
            to, how = (("UU", o + w * h, o + w * h + w), ALU.subtract) if sub else (tp, ALU.min)
            if d == 0:
                b = 256 * t + 64 * kap + f * h
                gat(CFG["g0"][kap], tp, win, ("H0", b, b + f))
                continue
            if d == 4 and kap == 0:
                gat("A", ("pD", w * h, w * h + w), win, off)
                tt(to, ("pD", w * h, w * h + w), rr, how)
            else:
                gat("V", to, win, off, rr, how)
            if sub:
                if d < 4:
                    act(rr, to, ACT.Abs, scale=KSUB)
                if CFG["te"][5 * kap + d] == "A":
                    act(tp, to, ACT.Relu)
                else:
                    ts(tp, to, 0.0, None, ALU.max)
        if d == 4:
            return
        if 0 < d <= CFG["acc"][kap]:
            c0, td = ("tp", 5120 * sl, 5120 * sl + 1024), ("tp", ot, ot + 1024)
            add("G", lambda: g.dma_start(ap(c0), ap(td), accum_op=ALU.add), [td, c0], [c0], 1000, sem="ac%d" % kap, lat=3500)
        for h in range(2):
            rr = ("RR", o + 512 * h, o + 512 * h + 512)
            if d == 0 or not sub:
                yb = bank("Y")
                it = [((yb, 0, 512), ("IS" if sub else "IK", 0, 128), ("tp", ot + 512 * h, ot + 512 * h + 512))]
                if d == 0:
                    an, a = ("A3" if sub else "A2"), 256 * t + 128 * h
                    it += [((yb, j, 512, 4), ("IB", 0, 128), (an, a, a + 128)) for j in range(4)]
                else:
                    it = [((yb, 0, 512), ("IB", 0, 128), rr)] + it
                grp(it)
                act(rr, (yb, 0, 512), ACT.Relu)
            if sub:
                act(("RT", o + 512 * h, o + 512 * h + 512), rr, ACT.Relu, bias=("cf", 47, 48), scale=-1.0 / (TAU * KSUB ** d))
        whole = CFG["int"]
        first = ("hc0", 64, 128) if whole else ("hc0", 0, 64)
        hp = (bank("H"), 0, 64)
        old, new = first if d == 0 else sf(4 * (d % 2)), sf(4 * ((d + 1) % 2))
        it = [(hp, wz(t, 0, s), ("tp", ot + s, ot + 1024, 16)) for s in range(16)]
        hr = [(wz(t, 0, s), ("RT", o + s, o + 1024, 16)) if sub else (wz(t, 1, s), ("RR", o + s, o + 1024, 16)) for s in range(16)]
        si = [("si", 128 * sl, 128 * sl + 64), ("si", 128 * sl + 64, 128 * sl + 128)]
        if d == 3 and CFG["last1"] and not whole:
            grp([(hp, ("I32", 0, 128), old)] + it, stop=False)
            grp([(hp,) + hr[s] for s in range(16)], start=False)
        else:
            if CFG["hc"] == "A" and d == 0:
                grp(it)
                act(new, hp, ACT.Identity, bias=(first[0], first[1], first[1] + 1))
            elif CFG["hc"] == "A":
                grp([(hp, ("I32", 0, 128), old)] + it)
                act(new, hp, ACT.Copy)
            else:
                grp(it)
                tt(new, hp, old, ALU.add)
            hp = (bank("H"), 0, 64)
            grp(([] if whole else [(hp, ("I32", 0, 128), new)]) + [(hp,) + hr[s] for s in range(16)])
        if whole:
            tt(si[0], hp, new, ALU.add)
            ts(si[1], si[0], 4095, None, ALU.bitwise_and)
            ts(sf(2), si[1], -2047.5, None, ALU.add)
        else:
            fold(hp, sf(1), sf(2), CFG["fa"][kap])
        c = 24 + 4 * d + kap
        place(sf(2), ("cf", 12 + kap, 13 + kap), ("cf", c, c + 1), sf(3), sf(1), si[0], si[1], 4095, ("off", 64 * sl, 64 * sl + 64))

    def masks(t, kap):
        sl = kap % 3
        for h in range(2):
            yb = bank("C")
            for d in [0] + list(range(CFG["acc"][kap] + 1, 5)):
                grp([((yb, 0, 512), ("IB", 0, 128), ("tp", 5120 * kap + 1024 * d + 512 * h, 5120 * kap + 1024 * d + 512 * h + 512))],
                    start=(d == 0), stop=(d == 4))
            for e in range(3):
                o, mo = 3072 * sl + 1024 * e + 512 * h, 3072 * (t % 2) + 1024 * e + 512 * h
                tt(("cE", o, o + 512), (yb, 0, 512), ("MR", mo, mo + 512), ALU.mult)

    ring = [0]

    def verdict(t, kap):
        sl = kap % 3
        an, a0 = AT[t]
        DB = bank("D")
        mm([((DB, 0, 128), ("ones", 0, 128), ("half", 0, 128), True, False)])
        srcs = [lb(t, 3)[:2], (an, a0), lb(t, 0)[:2]]
        for h in range(2):
            for e in range(3):
                xb = bank("X")
                ae = 512 * (ring[0] % 4)
                ring[0] += 1
                o = 3072 * sl + 1024 * e + 512 * h
                sn, s0 = srcs[e]
                grp([((xb, 0, 512), ("QB", 256 * t, 256 * t + 128), ("cE", o, o + 512))], stop=False)
                grp([((xb, j, 512, 4), ("QB", 256 * t, 256 * t + 128), (sn, s0 + 128 * h, s0 + 128 * h + 128)) for j in range(4)], start=False)
                act(("aE", ae, ae + 512), (xb, 0, 512), ACT.Abs, bias=("NT", t, t + 1))
                for b0 in (0, 2):
                    mm([((DB, 64 * h + 16 * b, 64 * h + 16 * b + 16), ("aE", ae + 128 * b, ae + 128 * b + 128), ("RD", 16 * e, 16 * e + 16),
                         False, h == 1 and e == 2 and b == 3) for b in (b0, b0 + 1)])
        t1 = ("t1", 64 * sl, 64 * sl + 64)
        ts(t1, (DB, 0, 128, 2), -2.0 ** 22, 0.0, ALU.mult, ALU.min)
        tt(("NW", 64 * kap, 64 * kap + 64), (DB, 1, 128, 2), t1, ALU.is_lt)

    def tail(t):
        an, a0 = AT[t]
        mm([(("PS5", 0, 256), ("BDB", 0, 128), ("ntm", 256 * t, 256 * t + 256), True, False)])
        grp([(("PS4", 0, 32, 1, 64), ("NW", 64 * j, 64 * j + 64), ("SEL", 0, 32)) for j in range(4)])
        act(("cnt", 0, 32, 1, 64), ("PS4", 0, 32, 1, 64), ACT.Copy)
        grp([(("PS5", 32 * j, 32 * j + 32), ("BC", 128 * j, 128 * j + 128, 1, 64), ("cnt", 0, 32, 1, 64)) for j in range(8)], start=False)
        ts(lb(t, 5), ("PS5", 0, 256), 0.0, None, ALU.is_gt)
        tt(lb(t, 6), lb(t, 5), lb(t, 4), ALU.mult)
        if t < 2:
            sca((BT[t][0], 2048, 4352), ("lu", 32 * t + 16, 32 * t + 32), lb(t, 6), lb(t, 0))
        else:
            tt(("RES", 256, 512), lb(t, 6), lb(t, 0), ALU.add)
        tt(lb(t, 1), lb(t, 5), lb(t, 2), ALU.mult)
        tt((an, a0, a0 + 256) if t < 2 else ("RES", 0, 256), lb(t, 1), (an, a0, a0 + 256), ALU.add)

    prep_q(0, "PS5")
    for t in range(3):
        if t == 1:
            send([(2, ("TB", 2048, 4096), ("TC", 2048, 4096), "rB1")], 8000)
            send([(2, ("TB", 512, 2048), ("TC", 512, 2048), "rR1")], 14000)
            send([(2, ("TB", 0, 256), ("TC", 0, 256), "rS1")], 15000)
        if t == 2:
            send([(-1, ("TC", 2048, 4096), ("TD", 0, 2048), "rB2")], 8000)
            send([(1, ("TC", 2048, 4096), ("TE", 0, 2048), "rE2")], 15000)
            send([(1, ("TC", 0, 512), ("TF", 0, 512), "rF2")], 17000)
            store("S", "y1", lambda: T.y[:, 0:512], ("TF", 0, 512), 3000)
        units = [(CFG["start"][kap] + d * CFG["pace"][kap], kap, d) for kap in range(4) for d in range(5)]
        if t == 0:
            units.append((CFG["pr0"], 4, 0))
        if t < 2:
            units += [(CFG["pq"], 5, 0), (CFG["pr"], 4, t + 1)]
        for (_, kap, d) in sorted(units):
            tag[0] = kap
            if kap == 4:
                prep_r(d, bank("H"))
            elif kap == 5:
                prep_q(t + 1, bank("H"))
            else:
                step(t, kap, d)
            if d < 4 or kap > 3:
                continue
            if kap == 0:
                tag[0] = 11
                prep_b(t)
                tt(lb(t, 4), ("pD", 0, 1024, 4), lb(t, 0), ALU.subtract)
            tag[0] = 12 + kap
            masks(t, kap)
            tag[0] = 6 + kap
            verdict(t, kap)
        tag[0] = 10
        tail(t)
    send([(-2, ("RES", 0, 512), ("RESL", 0, 512), "rRes")], 4000)
    sca(("TE", 0, 2304), ("OFL", 0, 16), ("RESL", 256, 512))
    store("S", "y2", lambda: T.y[:, 2048:4096], ("TE", 0, 2048), 4500)
    store("A", "y3", lambda: T.y[:, 512:768], ("RESL", 0, 256), 2500)
    return ops, eng


def depend(ops):
    n = len(ops)
    deps = [dict() for _ in range(n)]
    hist = {}
    for i, o in enumerate(ops):
        acc = [(r, False) for r in o["rd"]] + [(r, True) for r in o["wr"]]
        for r, w in acc:
            ps = r[0].startswith("PS")
            for (j, lo, hi, w2, st) in hist.get(r[0], []):
                if j == i:
                    continue
                same = ops[j]["e"] == o["e"] and "sem" not in ops[j] and "remote" not in ops[j] and "sem" not in o and "remote" not in o
                over = lo < r[2] and r[1] < hi
                if same and len(r) > 3 and st == r[3] and (lo - r[1]) % st:
                    over = False
                if ps and not same:
                    deps[i][j] = True
                elif ps:
                    deps[i].setdefault(j, False)
                elif over and (w or w2):
                    if (not same) or (w2 and not w) or CFG.get("strict"):
                        deps[i][j] = True
                    else:
                        deps[i].setdefault(j, False)
        for r, w in acc:
            h = hist.setdefault(r[0], [])
            if r[0].startswith("PS"):
                h[:] = []
            elif w and len(r) <= 3:
                h[:] = [x for x in h if not (r[1] <= x[1] and x[2] <= r[2]) or x[0] == i]
            h.append((i, r[1], r[2], w, r[3] if len(r) > 3 else 1))
        if "after" in o:
            deps[i][o["after"]] = False
    last = None
    for i, o in enumerate(ops):
        if "remote" in o:
            if last is not None:
                deps[i].setdefault(last, False)
            last = i
    return deps


def plan(ops, deps=None):
    n = len(ops)
    if deps is None:
        deps = depend(ops)
    succ = [[] for _ in range(n)]
    for i in range(n):
        for j in deps[i]:
            succ[j].append(i)
    full = [o["cost"] + o.get("lat", 0) for o in ops]
    pri = [0.0] * n
    for i in range(n - 1, -1, -1):
        pri[i] = full[i] + max([pri[s] + (HOP if deps[s][i] else 0) for s in succ[i]] + [0.0])
    left = [len(deps[i]) for i in range(n)]
    ready = [0.0] * n
    fin = [0.0] * n
    free = {e: 0.0 for e in "VAPGSX"}
    pool = {e: [] for e in "VAPGSX"}
    for i in range(n):
        if not left[i]:
            pool[ops[i]["e"]].append(i)
    order = []
    look = CFG["look"]
    rank = [pri[x] + CFG["bonus"][ops[x]["tag"]] for x in range(n)]
    for _ in range(n):
        best = None
        for e in pool:
            if pool[e]:
                st = max(free[e], min(ready[i] for i in pool[e]))
                if best is None or st < best[0]:
                    best = (st, e)
        st, e = best
        i = max((x for x in pool[e] if ready[x] <= st), key=lambda x: (rank[x], -x))
        soon = [x for x in pool[e] if st < ready[x] <= st + min(look, CFG["frac"] * ops[i]["cost"]) and rank[x] > rank[i] + CFG["gap"]]
        if soon:
            i = min(soon, key=lambda x: (ready[x], -rank[x]))
        st = max(st, ready[i])
        pool[e].remove(i)
        free[e] = st + ops[i]["cost"]
        fin[i] = st + full[i]
        order.append(i)
        for s in succ[i]:
            ready[s] = max(ready[s], fin[i] + HOP if deps[s][i] or ops[s]["e"] == "X" else st + ops[i]["cost"])
            left[s] -= 1
            if not left[s]:
                pool[ops[s]["e"]].append(s)
    sig = [False] * n
    known = {e: {} for e in "VAPGS"}
    pos = {}
    for p_, i in enumerate(order):
        pos[i] = p_
    clock = [None] * n
    waits = [[] for _ in range(n)]
    for i in order:
        o = ops[i]
        e = o["e"]
        if e == "X":
            clock[i] = {}
            continue
        kn = known[e]
        need = sorted([j for j in deps[i] if deps[i][j]], key=lambda j: -pos[j])
        for j in need:
            key = ops[j].get("sem", ops[j]["e"])
            if kn.get(key, -1) >= pos[j]:
                continue
            waits[i].append(j)
            sig[j] = True
            kn[key] = pos[j]
            for a, b in clock[j].items():
                if kn.get(a, -1) < b:
                    kn[a] = b
        clock[i] = dict(kn)
    return order, waits, sig, max(fin), fin


def rank_program(g, core, T, topo):
    if T.rank_of(core) is None:
        return
    ops, eng = build(g, core, T, topo)
    if "plan" not in CACHE:
        CACHE["plan"] = plan(ops)
    order, waits, sig = CACHE["plan"][:3]
    count = {"V": 0, "A": 0, "P": 0, "G": 0}
    mark = {}
    total = {}
    sent = 0
    for i in order:
        o = ops[i]
        e = o["e"]
        if e == "X":
            mark[i] = (o["sem"], o["n"])
            total[o["sem"]] = o["n"]
            continue
        for j in waits[i]:
            eng[e].wait_ge(T.sem[mark[j][0]], mark[j][1])
        r = o["fn"]()
        if "remote" in o:
            sent += o["remote"]
        elif "sem" in o:
            r.then_inc(T.sem[o["sem"]], 16)
            total[o["sem"]] = total.get(o["sem"], 0) + 16
            mark[i] = (o["sem"], total[o["sem"]])
        elif sig[i]:
            count[e] += 1
            r.then_inc(T.sem[CSEM[e]], 1)
            mark[i] = (CSEM[e], count[e])
    for e in count:
        if count[e]:
            g.wait_ge(T.sem[CSEM[e]], count[e])
    g.wait_ge(T.sem.sent, sent)
    for s in total:
        g.wait_ge(T.sem[s], total[s])
